import numpy as np
import ml_dtypes


def mxq(x, axis, fmt="e4m3"):
    dtype, down = {"e4m3": (ml_dtypes.float8_e4m3fn, 7), "e5m2": (ml_dtypes.float8_e5m2, 14)}[fmt]
    v = np.moveaxis(np.asarray(x, np.float32).astype(ml_dtypes.bfloat16).astype(np.float64), axis, -1)
    blocks = v.reshape(v.shape[:-1] + (-1, 32))
    amax = np.abs(blocks).max(-1, keepdims=True)
    byte = np.maximum(np.where(amax > 0, np.frexp(amax)[1] - 1 + 127, 0) - down, 1)
    scale = np.exp2(byte - 127.0)
    codes = (blocks / scale).astype(np.float32).astype(dtype).astype(np.float64)
    return np.moveaxis((codes * scale).reshape(v.shape), -1, axis)


WIDE = False


def mx_kscale(k):
    if not WIDE:
        return np.ones(k)
    levels = np.array([10, -10, 5, -5, 0])
    if k % 512:
        return np.exp2(np.random.permutation(np.resize(levels, k // 32))).repeat(32)
    a = np.empty((k // 512, 16))
    for p in range(k // 512):
        a[p, :8] = np.random.permutation(np.resize(levels, 8))
        for g in range(8):
            far = levels[np.abs(levels - a[p, g]) >= 10]
            a[p, g + 8] = far[np.random.randint(len(far))]
    return np.exp2(a.ravel()).repeat(32)


BF16 = ml_dtypes.bfloat16


def bf(x):
    return np.asarray(x, np.float32).astype(BF16)


def f64(x):
    return np.asarray(x).astype(np.float64)


E2M1 = np.array([0.0, 0.5, 1.0, 1.5, 2.0, 3.0, 4.0, 6.0, -0.0, -0.5, -1.0, -1.5, -2.0, -3.0, -4.0, -6.0])


def pack_weight(w, fmt):
    k, n = w.shape
    w = f64(bf(w)).reshape(k // 32, 32, n)
    amax = np.abs(w).max(1)
    if fmt == "e4m3":
        byte = np.frexp(amax)[1] - 1 + 127 - 7
    else:
        mant, ex = np.frexp(amax / 6.0)
        byte = np.where(mant > 0.5, ex, ex - 1) + 127
    byte = np.clip(np.where(amax > 0, byte, 1), 1, 254)
    scaled = (w * np.exp2(127.0 - byte)[:, None, :]).reshape(k, n).astype(np.float32)
    by_word = np.ascontiguousarray(scaled.reshape(k // 512, 128, 4, n).transpose(0, 1, 3, 2))
    if fmt == "e4m3":
        words = by_word.astype(ml_dtypes.float8_e4m3fn).view(np.uint8)
    else:
        c = by_word.astype(ml_dtypes.float4_e2m1fn).view(np.uint8) & 0xF
        words = c[..., 0::2] | (c[..., 1::2] << 4)
    return np.ascontiguousarray(words), np.ascontiguousarray(byte.astype(np.uint8).reshape(k // 512, 16, n))


def unpack_weight(words, scales, fmt):
    g, p, n, _ = words.shape
    if fmt == "e4m3":
        vals = np.ascontiguousarray(words).view(ml_dtypes.float8_e4m3fn).astype(np.float64)
    else:
        nib = np.empty((g, p, n, 4), np.uint8)
        nib[..., 0::2] = words & 0xF
        nib[..., 1::2] = words >> 4
        vals = E2M1[nib]
    vals = vals * np.repeat(np.exp2(scales.astype(np.float64) - 127.0), 8, axis=1)[..., None]
    return vals.transpose(0, 1, 3, 2).reshape(g * 512, n)
def pack4(w):
    words, scales = pack_weight(w, "e2m1")
    return words.reshape(words.shape[0], 128, -1), scales


def unpack4(words, scales):
    return unpack_weight(words.reshape(words.shape[0], 128, -1, 2), scales, "e2m1")


E4M3FN = np.array([(-1.0 if i & 128 else 1.0) * ((1.0 + (i & 7) / 8.0) * 2.0 ** (((i >> 3) & 15) - 7) if i & 120 else (i & 7) * 2.0 ** -9) for i in range(256)])


def e4m3fn_bytes(y):
    return np.clip(np.asarray(y, np.float64), -448.0, 448.0).astype(np.float32).astype(ml_dtypes.float8_e4m3fn).view(np.uint8)


def e4m3fn_values(b):
    return E4M3FN[b]


B, N, D, F, G, C = 4, 64, 2048, 512, 512, 3
F2 = 2 * F


def _sigmoid(y):
    return 1.0 / (1.0 + np.exp(-y))


def _silu(y):
    return y * _sigmoid(y)


def _pair_sq_dist(pos):
    diff = pos[:, :, None, :] - pos[:, None, :, :]
    return np.sum(diff * diff, axis=-1)


def draw0():
    s, t = mx_kscale(D), mx_kscale(F)
    h = bf(np.random.standard_normal((B, N, D)) * s)
    pos = bf(np.random.standard_normal((B, N, C)))
    w1_words, w1_scales = pack4(np.random.standard_normal((D, F2)) / np.sqrt(D) / s[:, None])
    wr = bf(np.random.standard_normal(F) * 0.2)
    edge_gain = bf((1.0 + 0.1 * np.random.standard_normal(F)) * t)
    w2_words, w2_scales = pack4(np.random.standard_normal((F, G)) / np.sqrt(F) / t[:, None])
    gate_w = bf(np.random.standard_normal(G) / np.sqrt(G))
    return {
        "h": h,
        "pos": pos,
        "w1_words": w1_words,
        "w1_scales": w1_scales,
        "wr": wr,
        "edge_gain": edge_gain,
        "w2_words": w2_words,
        "w2_scales": w2_scales,
        "gate_w": gate_w,
    }


def core(h, pos, w1_words, w1_scales, wr, edge_gain, w2_words, w2_scales, gate_w):
    w2 = unpack4(w2_words, w2_scales)
    b, n, _ = h.shape
    f = w2.shape[0]

    uv = mxq(f64(h), 2, "e4m3") @ unpack4(w1_words, w1_scales)
    u = uv[..., :f]
    v = uv[..., f:]

    r2 = _pair_sq_dist(f64(pos))

    pre = u[:, :, None, :] + v[:, None, :, :] + r2[..., None] * f64(wr)

    a = _silu(pre) * f64(edge_gain)

    rows = a.reshape(b * n * n, f)
    m = _silu(mxq(rows, 1, "e4m3") @ w2).reshape(b, n, n, w2.shape[1])

    g = _sigmoid(np.sum(m * f64(gate_w), axis=-1))

    return np.sum(g[..., None] * m, axis=2) / np.sqrt(n)


def setup_inputs():
    drawn = draw0()
    full = np.asarray(drawn['h']).astype(np.float64)
    scale = (np.abs(full).reshape(4, 64, 16, 128).max(axis=(3,)) / 448.0).astype(np.float32)
    given = {}
    for key, value in drawn.items():
        if key == 'h':
            given['h_bytes'] = e4m3fn_bytes(full / np.repeat(scale.astype(np.float64), 128, axis=2))
            given['h_scale'] = scale
        else:
            given[key] = value
    return given


def reference(h_bytes, h_scale, pos, w1_words, w1_scales, wr, edge_gain, w2_words, w2_scales, gate_w):
    return core(e4m3fn_values(h_bytes) * np.repeat(h_scale.astype(np.float64), 128, axis=2), pos, w1_words, w1_scales, wr, edge_gain, w2_words, w2_scales, gate_w)

@@ -1,0 +1,333 @@
+from contextlib import ExitStack
+
+import concourse.mybir as mybir
+from concourse.masks import make_identity
+
+F32 = mybir.dt.float32
+BF16 = mybir.dt.bfloat16
+U32 = mybir.dt.uint32
+U8 = mybir.dt.uint8
+I32 = mybir.dt.int32
+FP8 = mybir.dt.float8_e4m3fn
+FP8X4 = mybir.dt.float8_e4m3fn_x4
+FP4X4 = mybir.dt.float4_e2m1fn_x4
+ACT = mybir.ActivationFunctionType
+ALU = mybir.AluOpType
+AX = mybir.AxisListType
+
+FLOPS = 2 * 256 * 2048 * 1024 + 2 * 16384 * 512 * 512
+
+P = 128
+GRAPHS, NODES, DEPTH, FEAT, CHAN = 4, 64, 2048, 512, 512
+ROWS = GRAPHS * NODES
+GROUPS = DEPTH // 512
+T4 = 4
+TILES = GRAPHS * NODES * NODES // P
+PER_GRAPH = TILES // GRAPHS
+BLOCKS = TILES // 4
+
+
+def tile_egnngatededgelayer_d1p_kernel(
+    tc, h_bytes, h_scale, pos, w1_words, w1_scales, wr, edge_gain, w2_words, w2_scales, gate_w, out
+):
+    nc = tc.nc
+    with ExitStack() as ctx:
+        keep = ctx.enter_context(tc.tile_pool(name="keep", bufs=1))
+        work = ctx.enter_context(tc.tile_pool(name="work", bufs=2))
+        psum = ctx.enter_context(tc.psum_pool(name="psum", bufs=2))
+        ctx.enter_context(tc.manual_schedule())
+
+        def bank(tag, bufs):
+            ps_tile = psum.tile([P, 512], F32, name=tag, tag=tag, bufs=bufs)
+            return ps_tile
+
+        hb = [keep.tile([P, DEPTH], U8, name=f"hb{r}") for r in range(2)]
+        hs = keep.tile([P, 2, 16], F32, name="hs")
+        h_rows = h_bytes.flatten_outer_dims()
+        for r in range(2):
+            nc.sync.dma_start(out=hb[r][:], in_=h_rows[r * P : (r + 1) * P, :])
+            if r == 0:
+                nc.sync.dma_start(out=hs[:], in_=h_scale.flatten_outer_dims().rearrange("(r p) k -> p r k", p=P))
+
+        w1s = keep.tile([P, GROUPS, 1024], U8, name="w1s", align_bytes=64)
+        w2s = keep.tile([P, CHAN], U8, name="w2s", align_bytes=64)
+        nc.gpsimd.memset(w1s[:].rearrange("p g n -> p (g n)").bitcast(I32), 0)
+        nc.gpsimd.memset(w2s[:].bitcast(I32), 0)
+        w1w = keep.tile([P, GROUPS, 2048], U8, name="w1w", align_bytes=64)
+        w2w = keep.tile([P, 1024], U8, name="w2w", align_bytes=64)
+        w1s_dst = w1s[:].rearrange("p g n -> p (g n)").bitcast(I32).rearrange("p (g n) -> p g n", g=GROUPS)
+        for q in range(4):
+            nc.sync.dma_start(
+                out=w1s_dst[32 * q : 32 * q + 4],
+                in_=w1_scales.bitcast(I32)[:, 4 * q : 4 * q + 4, :].rearrange("g r n -> r g n"),
+            )
+        posb = keep.tile([P, GRAPHS * NODES * 3], BF16, name="posb")
+        posj = keep.tile([P, GRAPHS, 4], BF16, name="posj")
+        nc.gpsimd.dma_start(out=posb[:], in_=pos.rearrange("b n c -> (b n c)").partition_broadcast(P))
+        for half in range(2):
+            nc.gpsimd.dma_start(out=posj[64 * half : 64 * half + 64, :, 0:3], in_=pos.rearrange("b j c -> j b c"))
+        for g in range(GROUPS):
+            nc.sync.dma_start(
+                out=w1w[:, g, :].bitcast(I32), in_=w1_words[g].bitcast(I32)
+            )
+        wr_bf = keep.tile([P, T4], BF16, name="wr_bf")
+        gain_bf = keep.tile([P, T4], BF16, name="gain_bf")
+        nc.gpsimd.dma_start(out=wr_bf[:], in_=wr.rearrange("(p t) -> p t", t=T4))
+        nc.gpsimd.dma_start(out=gain_bf[:], in_=edge_gain.rearrange("(p t) -> p t", t=T4))
+        nc.sync.dma_start(out=w2w[:].bitcast(I32), in_=w2_words[0].bitcast(I32))
+        for q in range(4):
+            nc.sync.dma_start(
+                out=w2s[32 * q : 32 * q + 4, :].bitcast(I32),
+                in_=w2_scales[0].bitcast(I32)[4 * q : 4 * q + 4, :],
+            )
+        gw = keep.tile([P, CHAN], BF16, name="gw")
+        nc.sync.dma_start(out=gw[:], in_=gate_w.partition_broadcast(P))
+
+        warm = keep.tile([P, 1], F32, name="warm")
+        nc.vector.memset(warm[:], 0.0)
+        nc.scalar.activation(warm[:], warm[:], ACT.Silu)
+        ident = keep.tile([P, P], F32, name="ident")
+        make_identity(nc, ident[:])
+        mask = keep.tile([P, 2], F32, name="mask")
+        nc.vector.memset(mask[:], 0.0)
+        nc.vector.memset(mask[0:64, 0:1], 0.0625)
+        nc.vector.memset(mask[64:128, 1:2], 0.0625)
+
+        hbf = [keep.tile([P, DEPTH], BF16, name=f"hbf{r}") for r in range(2)]
+        for r in range(2):
+            for kb in range(16):
+                cols = slice(kb * 128, kb * 128 + 128)
+                if kb % 2 == 0:
+                    nc.vector.tensor_scalar(
+                        hbf[r][:, cols], hb[r][:, cols].bitcast(FP8), hs[:, r, kb : kb + 1], None, ALU.mult
+                    )
+                else:
+                    nc.scalar.activation(
+                        hbf[r][:, cols], hb[r][:, cols].bitcast(FP8), ACT.Copy, scale=hs[:, r, kb : kb + 1]
+                    )
+
+        wr_f = keep.tile([P, T4], F32, name="wr_f")
+        gain_f = keep.tile([P, T4], F32, name="gain_f")
+        nc.vector.tensor_copy(wr_f[:], wr_bf[:])
+        nc.vector.tensor_copy(gain_f[:], gain_bf[:])
+        diff = keep.tile([P, TILES, 3], F32, name="diff")
+        posb_v = posb[:].rearrange("p (b s i c) -> p b s i c", b=GRAPHS, i=2, c=3)
+        for b in range(GRAPHS):
+            for half in range(2):
+                rows = slice(64 * half, 64 * half + 64)
+                nc.vector.tensor_tensor(
+                    diff[rows, b * PER_GRAPH : (b + 1) * PER_GRAPH, :],
+                    posb_v[rows, b, :, half, :],
+                    posj[rows, b, 0:3].unsqueeze(1).to_broadcast([64, PER_GRAPH, 3]),
+                    ALU.subtract,
+                )
+        nc.vector.tensor_tensor(diff[:], diff[:], diff[:], ALU.mult)
+        r2 = keep.tile([P, TILES], F32, name="r2")
+        nc.vector.tensor_reduce(r2[:], diff[:], AX.X, ALU.add)
+
+        hcodes = keep.tile([P, GROUPS, ROWS], U32, name="hcodes", align_bytes=64)
+        hplane = keep.tile([P, GROUPS, ROWS], U8, name="hplane", align_bytes=64)
+        hq = keep.tile([P, GROUPS, ROWS * 4], BF16, name="hq", align_bytes=64)
+        uv = [[bank("mx", 4) for half in range(2)] for r in range(2)]
+        xts = []
+        for g in range(GROUPS):
+            xt = bank("r2" if g % 2 == 0 else "o", 2)
+            xts.append(xt)
+            xv = xt[:].rearrange("p (r u x) -> p r u x", r=2, u=2)
+            for r in range(2):
+                words = hbf[r][:].bitcast(F32)
+                for u in range(2):
+                    nc.tensor.transpose(xv[:, r, u, :], words[:, 256 * g + u : 256 * (g + 1) : 2], ident[:])
+        for g in range(GROUPS):
+            dst = hq[:, g, :].bitcast(F32).rearrange("p (r x u) -> p r x u", r=2, u=2)
+            src = xts[g][:].rearrange("p (r u x) -> p r x u", r=2, u=2)
+            if g % 2 == 0:
+                nc.vector.tensor_copy(dst, src)
+            else:
+                nc.scalar.copy(dst, src)
+        for g in range(GROUPS):
+            nc.vector.quantize_mx(out=hcodes[:, g, :].bitcast(FP8X4), scales=hplane[:, g, :], in_=hq[:, g, :])
+        for g in range(GROUPS):
+            for r in range(2):
+                for half in range(2):
+                    nc.tensor.matmul_mx(
+                        out=uv[r][half][:],
+                        lhsT=hcodes[:, g, r * P : (r + 1) * P].bitcast(FP8X4),
+                        lhsT_scale=hplane[:, g, r * P : (r + 1) * P],
+                        rhs=w1w[:, g, half * 1024 : (half + 1) * 1024].bitcast(FP4X4),
+                        rhs_scale=w1s[:, g, half * 512 : (half + 1) * 512],
+                        start=(g == 0),
+                        stop=(g == GROUPS - 1),
+                    )
+        uT = keep.tile([P, T4, ROWS], F32, name="uT")
+        vT = keep.tile([P, T4, ROWS], F32, name="vT")
+        uvrow = keep.tile([P, 2, 2, T4, P], F32, name="uvrow")
+        for r in range(2):
+            for half in range(2):
+                src = uv[r][half][:].rearrange("p (m t) -> p t m", t=T4)
+                if half == 0:
+                    nc.vector.tensor_copy(uvrow[:, r, half], src)
+                else:
+                    nc.scalar.copy(uvrow[:, r, half], src)
+        for r in range(2):
+            for half in range(2):
+                tp = bank("r2" if half == 0 else "o", 2)
+                for t in range(T4):
+                    nc.tensor.transpose(tp[:, t * P : (t + 1) * P], uvrow[:, r, half, t, :], ident[:])
+                src = tp[:].rearrange("p (t x) -> p t x", t=T4)
+                if half == 0:
+                    nc.scalar.copy(uT[:, :, r * P : (r + 1) * P], src)
+                else:
+                    nc.vector.tensor_copy(vT[:, :, r * P : (r + 1) * P], src)
+
+        state = {}
+
+        def spread_r2(k):
+            ps = bank("r2", 2)
+            for q in range(4):
+                c = 4 * k + q
+                nc.tensor.transpose(ps[:, q * P : (q + 1) * P], r2[:, c : c + 1].to_broadcast([P, P]), ident[:])
+            state["r2", k] = ps
+
+        def pre(k):
+            b = k // 8
+            w = work.tile([P, T4, 512], F32, name="w", tag="w")
+            ps = state["r2", k]
+            for t in range(T4):
+                nc.vector.scalar_tensor_tensor(
+                    w[:, t, :].rearrange("p (i j) -> p i j", j=NODES),
+                    ps[:].rearrange("p (i j) -> p i j", j=NODES),
+                    wr_f[:, t : t + 1],
+                    vT[:, t, b * NODES : (b + 1) * NODES].unsqueeze(1).to_broadcast([P, 8, NODES]),
+                    ALU.mult,
+                    ALU.add,
+                )
+            state["w", k] = w
+
+        def silu1(k):
+            w = state["w", k]
+            s = work.tile([P, T4, 512], F32, name="s", tag="s")
+            for t in range(T4):
+                for i in range(8):
+                    e = slice(i * NODES, (i + 1) * NODES)
+                    node = k * 8 + i
+                    nc.scalar.activation(s[:, t, e], w[:, t, e], ACT.Silu, bias=uT[:, t, node : node + 1])
+            state["s", k] = s
+
+        def gain(k):
+            a = work.tile([P, 2048], BF16, name="a", tag="a", align_bytes=64)
+            nc.vector.tensor_tensor(
+                a[:].rearrange("p (e t) -> p e t", t=T4),
+                state["s", k][:].rearrange("p t e -> p e t"),
+                gain_f[:].unsqueeze(1).to_broadcast([P, 512, T4]),
+                ALU.mult,
+            )
+            state["a", k] = a
+
+        def quant(k):
+            codes = work.tile([P, 512], U32, name="codes", tag="codes", align_bytes=64)
+            plane = work.tile([P, 512], U8, name="plane", tag="plane", align_bytes=64)
+            nc.vector.quantize_mx(out=codes[:].bitcast(FP8X4), scales=plane[:], in_=state["a", k][:])
+            state["q", k] = (codes, plane)
+
+        def product(k):
+            codes, plane = state["q", k]
+            banks = []
+            for q in range(4):
+                ps = bank("mx", 4)
+                nc.tensor.matmul_mx(
+                    out=ps[:],
+                    lhsT=codes[:, q * P : (q + 1) * P].bitcast(FP8X4),
+                    lhsT_scale=plane[:, q * P : (q + 1) * P],
+                    rhs=w2w[:].bitcast(FP4X4),
+                    rhs_scale=w2s[:],
+                    start=True,
+                    stop=True,
+                )
+                banks.append(ps)
+            state["mx", k] = banks
+
+        def silu2(k):
+            m = work.tile([P, 4, CHAN], F32, name="m", tag="m", bufs=3)
+            for q in range(4):
+                nc.scalar.activation(m[:, q, :], state["mx", k][q][:], ACT.Silu)
+            state["m", k] = m
+
+        def gate_dot(k):
+            dot = work.tile([P, 4], F32, name="dot", tag="dot")
+            for q in range(4):
+                junk = work.tile([P, CHAN], F32, name="junk", tag="junk")
+                nc.vector.scalar_tensor_tensor(
+                    junk[:], state["m", k][:, q, :], 1.0, gw[:], ALU.mult, ALU.mult, accum_out=dot[:, q : q + 1]
+                )
+            state["dot", k] = dot
+
+        def gate_tanh(k):
+            th = work.tile([P, 4], F32, name="th", tag="th")
+            nc.scalar.activation(th[:], state["dot", k][:], ACT.Tanh, scale=0.5)
+            state["th", k] = th
+
+        def gate_cols(k):
+            gc = work.tile([P, 4, 2], F32, name="gc", tag="gc")
+            nc.vector.scalar_tensor_tensor(
+                gc[:],
+                state["th", k][:].unsqueeze(2).to_broadcast([P, 4, 2]),
+                1.0,
+                mask[:].unsqueeze(1).to_broadcast([P, 4, 2]),
+                ALU.add,
+                ALU.mult,
+            )
+            state["gc", k] = gc
+
+        def sums(k):
+            if k % 16 == 0:
+                state["o"] = bank("o", 2)
+            acc = state["o"][:].rearrange("p (s x) -> p s x", s=4)
+            for q in range(4):
+                col = 2 * ((4 * k + q) % 64)
+                for s in range(4):
+                    nc.tensor.matmul(
+                        acc[:, s, col : col + 2],
+                        lhsT=state["m", k][:, q, s * P : (s + 1) * P],
+                        rhs=state["gc", k][:, q, :],
+                        start=True,
+                        stop=True,
+                    )
+
+        def finish(k):
+            part = k // 16
+            oT = work.tile([P, 512], F32, name="oT", tag="oT")
+            nc.scalar.copy(oT[:], state["o"][:])
+            ps = bank("r2", 2)
+            for s in range(4):
+                nc.tensor.transpose(ps[:, s * P : (s + 1) * P], oT[:, s * P : (s + 1) * P], ident[:])
+            res = work.tile([P, CHAN], F32, name="res", tag="res")
+            nc.vector.tensor_copy(res[:], ps[:])
+            nc.sync.dma_start(out=out.flatten_outer_dims()[part * P : (part + 1) * P, :], in_=res[:])
+
+        spread_r2(0)
+        pre(0)
+        silu1(0)
+        spread_r2(1)
+        for k in range(BLOCKS + 2):
+            if k + 1 < BLOCKS:
+                pre(k + 1)
+            if 2 <= k:
+                gate_cols(k - 2)
+                sums(k - 2)
+            if 1 <= k <= BLOCKS:
+                silu2(k - 1)
+            if k + 1 < BLOCKS:
+                silu1(k + 1)
+            if k + 2 < BLOCKS:
+                spread_r2(k + 2)
+            if k < BLOCKS:
+                gain(k)
+            if 1 <= k <= BLOCKS:
+                gate_dot(k - 1)
+                gate_tanh(k - 1)
+            if k < BLOCKS:
+                quant(k)
+                product(k)
+            if 2 <= k and (k - 2) % 16 == 15:
+                finish(k - 2)

@@ -88,10 +88,14 @@ def tile_egnngatededgelayer_d1p_kernel(
         nc.scalar.activation(warm[:], warm[:], ACT.Silu)
         ident = keep.tile([P, P], F32, name="ident")
         make_identity(nc, ident[:])
-        mask = keep.tile([P, 2], F32, name="mask")
-        nc.vector.memset(mask[:], 0.0)
-        nc.vector.memset(mask[0:64, 0:1], 0.0625)
-        nc.vector.memset(mask[64:128, 1:2], 0.0625)
+        ident_bf = keep.tile([P, P], BF16, name="ident_bf")
+        nc.gpsimd.tensor_copy(ident_bf[:], ident[:])
+        first_row = keep.tile([P, P], BF16, name="first_row")
+        nc.vector.memset(first_row[:], 0.0)
+        nc.vector.memset(first_row[0:1, :], 1.0)
+        consts = psum.tile([P, 1024], BF16, name="consts", tag="consts", bufs=1)
+        gw_ps = consts[:, 0:CHAN]
+        gain_ps = consts[:, CHAN : CHAN + T4]
 
         hbf = [keep.tile([P, DEPTH], BF16, name=f"hbf{r}") for r in range(2)]
         for r in range(2):
@@ -107,9 +111,7 @@ def tile_egnngatededgelayer_d1p_kernel(
                     )
 
         wr_f = keep.tile([P, T4], F32, name="wr_f")
-        gain_f = keep.tile([P, T4], F32, name="gain_f")
         nc.vector.tensor_copy(wr_f[:], wr_bf[:])
-        nc.vector.tensor_copy(gain_f[:], gain_bf[:])
         diff = keep.tile([P, TILES, 3], F32, name="diff")
         posb_v = posb[:].rearrange("p (b s i c) -> p b s i c", b=GRAPHS, i=2, c=3)
         for b in range(GRAPHS):
@@ -128,10 +130,9 @@ def tile_egnngatededgelayer_d1p_kernel(
         hcodes = keep.tile([P, GROUPS, ROWS], U32, name="hcodes", align_bytes=64)
         hplane = keep.tile([P, GROUPS, ROWS], U8, name="hplane", align_bytes=64)
         hq = keep.tile([P, GROUPS, ROWS * 4], BF16, name="hq", align_bytes=64)
-        uv = [[bank("mx", 4) for half in range(2)] for r in range(2)]
         xts = []
         for g in range(GROUPS):
-            xt = bank("r2" if g % 2 == 0 else "o", 2)
+            xt = bank("mx", 4)
             xts.append(xt)
             xv = xt[:].rearrange("p (r u x) -> p r u x", r=2, u=2)
             for r in range(2):
@@ -147,6 +148,7 @@ def tile_egnngatededgelayer_d1p_kernel(
                 nc.scalar.copy(dst, src)
         for g in range(GROUPS):
             nc.vector.quantize_mx(out=hcodes[:, g, :].bitcast(FP8X4), scales=hplane[:, g, :], in_=hq[:, g, :])
+        uv = [[bank("mx", 4) for half in range(2)] for r in range(2)]
         for g in range(GROUPS):
             for r in range(2):
                 for half in range(2):
@@ -171,7 +173,7 @@ def tile_egnngatededgelayer_d1p_kernel(
                     nc.scalar.copy(uvrow[:, r, half], src)
         for r in range(2):
             for half in range(2):
-                tp = bank("r2" if half == 0 else "o", 2)
+                tp = bank("mx", 4)
                 for t in range(T4):
                     nc.tensor.transpose(tp[:, t * P : (t + 1) * P], uvrow[:, r, half, t, :], ident[:])
                 src = tp[:].rearrange("p (t x) -> p t x", t=T4)
@@ -180,10 +182,13 @@ def tile_egnngatededgelayer_d1p_kernel(
                 else:
                     nc.vector.tensor_copy(vT[:, :, r * P : (r + 1) * P], src)
 
+        nc.tensor.matmul(gw_ps, lhsT=first_row[:], rhs=gw[:], start=True, stop=True)
+        nc.tensor.matmul(gain_ps, lhsT=ident_bf[:], rhs=gain_bf[:], start=True, stop=True)
+
         state = {}
 
         def spread_r2(k):
-            ps = bank("r2", 2)
+            ps = bank("r2", 1)
             for q in range(4):
                 c = 4 * k + q
                 nc.tensor.transpose(ps[:, q * P : (q + 1) * P], r2[:, c : c + 1].to_broadcast([P, P]), ident[:])
@@ -198,7 +203,7 @@ def tile_egnngatededgelayer_d1p_kernel(
                     w[:, t, :].rearrange("p (i j) -> p i j", j=NODES),
                     ps[:].rearrange("p (i j) -> p i j", j=NODES),
                     wr_f[:, t : t + 1],
-                    vT[:, t, b * NODES : (b + 1) * NODES].unsqueeze(1).to_broadcast([P, 8, NODES]),
+                    uT[:, t, b * NODES : (b + 1) * NODES].unsqueeze(1).to_broadcast([P, 8, NODES]),
                     ALU.mult,
                     ALU.add,
                 )
@@ -211,7 +216,7 @@ def tile_egnngatededgelayer_d1p_kernel(
                 for i in range(8):
                     e = slice(i * NODES, (i + 1) * NODES)
                     node = k * 8 + i
-                    nc.scalar.activation(s[:, t, e], w[:, t, e], ACT.Silu, bias=uT[:, t, node : node + 1])
+                    nc.scalar.activation(s[:, t, e], w[:, t, e], ACT.Silu, bias=vT[:, t, node : node + 1])
             state["s", k] = s
 
         def gain(k):
@@ -219,7 +224,7 @@ def tile_egnngatededgelayer_d1p_kernel(
             nc.vector.tensor_tensor(
                 a[:].rearrange("p (e t) -> p e t", t=T4),
                 state["s", k][:].rearrange("p t e -> p e t"),
-                gain_f[:].unsqueeze(1).to_broadcast([P, 512, T4]),
+                gain_ps.unsqueeze(1).to_broadcast([P, 512, T4]),
                 ALU.mult,
             )
             state["a", k] = a
@@ -258,7 +263,7 @@ def tile_egnngatededgelayer_d1p_kernel(
             for q in range(4):
                 junk = work.tile([P, CHAN], F32, name="junk", tag="junk")
                 nc.vector.scalar_tensor_tensor(
-                    junk[:], state["m", k][:, q, :], 1.0, gw[:], ALU.mult, ALU.mult, accum_out=dot[:, q : q + 1]
+                    junk[:], state["m", k][:, q, :], 1.0, gw_ps, ALU.mult, ALU.mult, accum_out=dot[:, q : q + 1]
                 )
             state["dot", k] = dot
 
@@ -267,54 +272,70 @@ def tile_egnngatededgelayer_d1p_kernel(
             nc.scalar.activation(th[:], state["dot", k][:], ACT.Tanh, scale=0.5)
             state["th", k] = th
 
-        def gate_cols(k):
-            gc = work.tile([P, 4, 2], F32, name="gc", tag="gc")
-            nc.vector.scalar_tensor_tensor(
-                gc[:],
-                state["th", k][:].unsqueeze(2).to_broadcast([P, 4, 2]),
-                1.0,
-                mask[:].unsqueeze(1).to_broadcast([P, 4, 2]),
-                ALU.add,
-                ALU.mult,
-            )
-            state["gc", k] = gc
-
-        def sums(k):
-            if k % 16 == 0:
-                state["o"] = bank("o", 2)
-            acc = state["o"][:].rearrange("p (s x) -> p s x", s=4)
+        def weigh(k):
+            g = work.tile([P, 4], F32, name="g", tag="g")
+            nc.gpsimd.tensor_scalar(g[:], state["th", k][:], 1.0, 0.0625, ALU.add, ALU.mult)
+            gm = work.tile([P, 4, CHAN], F32, name="gm", tag="gm", bufs=8)
             for q in range(4):
-                col = 2 * ((4 * k + q) % 64)
-                for s in range(4):
+                nc.gpsimd.tensor_scalar(
+                    gm[:, q, :], state["m", k][:, q, :], g[:, q : q + 1], 0.0, ALU.mult, ALU.add
+                )
+            state["gm", k] = gm
+
+        def add_up(n, slices):
+            if 0 in slices:
+                state["acc", n] = bank("acc", 2)
+            acc = state["acc", n]
+            for s in slices:
+                for x in range(16):
                     nc.tensor.matmul(
-                        acc[:, s, col : col + 2],
-                        lhsT=state["m", k][:, q, s * P : (s + 1) * P],
-                        rhs=state["gc", k][:, q, :],
-                        start=True,
-                        stop=True,
+                        acc[:, s * P : (s + 1) * P],
+                        lhsT=state["gm", 4 * n + x // 4][:, x % 4, s * P : (s + 1) * P],
+                        rhs=ident[:],
+                        is_transpose=True,
+                        start=(x == 0),
+                        stop=(x == 15),
                     )
 
-        def finish(k):
-            part = k // 16
-            oT = work.tile([P, 512], F32, name="oT", tag="oT")
-            nc.scalar.copy(oT[:], state["o"][:])
-            ps = bank("r2", 2)
-            for s in range(4):
-                nc.tensor.transpose(ps[:, s * P : (s + 1) * P], oT[:, s * P : (s + 1) * P], ident[:])
-            res = work.tile([P, CHAN], F32, name="res", tag="res")
-            nc.vector.tensor_copy(res[:], ps[:])
-            nc.sync.dma_start(out=out.flatten_outer_dims()[part * P : (part + 1) * P, :], in_=res[:])
+        def collect(n):
+            b = n // 2
+            if n % 2 == 0:
+                part = work.tile([P, 512], F32, name="part", tag="part")
+                nc.vector.tensor_copy(part[:], state["acc", n][:])
+                state["part"] = part
+                return
+            both = work.tile([P, 4, 2, NODES], F32, name="both", tag="both")
+            nc.vector.tensor_tensor(
+                both[:].rearrange("p s h i -> p (s h i)"), state["acc", n][:], state["part"][:], ALU.add
+            )
+            if b % 2 == 0:
+                oT = work.tile([P, 4, 2, NODES], F32, name="oT", tag="oT")
+                state["oT"] = oT
+            oT = state["oT"]
+            nc.vector.tensor_tensor(oT[:, :, b % 2, :], both[:, :, 0, :], both[:, :, 1, :], ALU.add)
+            if b % 2 == 1:
+                ps = bank("r2", 1)
+                for s in range(4):
+                    nc.tensor.transpose(
+                        ps[:, s * P : (s + 1) * P], oT[:, s].rearrange("p b i -> p (b i)"), ident[:]
+                    )
+                res = work.tile([P, CHAN], F32, name="res", tag="res")
+                nc.scalar.copy(res[:], ps[:])
+                nc.sync.dma_start(out=out.flatten_outer_dims()[(b // 2) * P : (b // 2 + 1) * P, :], in_=res[:])
 
         spread_r2(0)
         pre(0)
         silu1(0)
         spread_r2(1)
-        for k in range(BLOCKS + 2):
+        for k in range(BLOCKS + 5):
             if k + 1 < BLOCKS:
                 pre(k + 1)
-            if 2 <= k:
-                gate_cols(k - 2)
-                sums(k - 2)
+            if 2 <= k < BLOCKS + 2:
+                weigh(k - 2)
+            if k % 4 == 2 and k >= 6:
+                add_up(k // 4 - 1, (0, 1))
+            if k % 4 == 3 and k >= 6:
+                add_up(k // 4 - 1, (2, 3))
             if 1 <= k <= BLOCKS:
                 silu2(k - 1)
             if k + 1 < BLOCKS:
@@ -326,8 +347,8 @@ def tile_egnngatededgelayer_d1p_kernel(
             if 1 <= k <= BLOCKS:
                 gate_dot(k - 1)
                 gate_tanh(k - 1)
+            if k % 4 == 0 and k >= 8:
+                collect(k // 4 - 2)
             if k < BLOCKS:
                 quant(k)
                 product(k)
-            if 2 <= k and (k - 2) % 16 == 15:
-                finish(k - 2)

@@ -37,6 +37,10 @@ def tile_egnngatededgelayer_d1p_kernel(
         psum = ctx.enter_context(tc.psum_pool(name="psum", bufs=2))
         ctx.enter_context(tc.manual_schedule())
 
+        def big(shape, dtype, label):
+            big_tile = work.tile(shape, dtype, name=label, tag="gm", bufs=9, align_bytes=64)
+            return big_tile
+
         def bank(tag, bufs):
             ps_tile = psum.tile([P, 512], F32, name=tag, tag=tag, bufs=bufs)
             return ps_tile
@@ -44,16 +48,27 @@ def tile_egnngatededgelayer_d1p_kernel(
         hb = [keep.tile([P, DEPTH], U8, name=f"hb{r}") for r in range(2)]
         hs = keep.tile([P, 2, 16], F32, name="hs")
         h_rows = h_bytes.flatten_outer_dims()
+        nc.scalar.dma_start(out=hs[:], in_=h_scale.flatten_outer_dims().rearrange("(r p) k -> p r k", p=P))
         for r in range(2):
             nc.sync.dma_start(out=hb[r][:], in_=h_rows[r * P : (r + 1) * P, :])
-            if r == 0:
-                nc.sync.dma_start(out=hs[:], in_=h_scale.flatten_outer_dims().rearrange("(r p) k -> p r k", p=P))
+        ident = keep.tile([P, P], F32, name="ident")
+        make_identity(nc, ident[:])
+
+        posb = keep.tile([P, GRAPHS * NODES * 3], BF16, name="posb")
+        posj = keep.tile([P, GRAPHS, 4], BF16, name="posj")
+        nc.scalar.dma_start(out=posb[:], in_=pos.rearrange("b n c -> (b n c)").partition_broadcast(P))
+        for half in range(2):
+            nc.scalar.dma_start(out=posj[64 * half : 64 * half + 64, :, 0:3], in_=pos.rearrange("b j c -> j b c"))
+        wr_bf = keep.tile([P, T4], BF16, name="wr_bf")
+        gain_bf = keep.tile([P, T4], BF16, name="gain_bf")
+        nc.scalar.dma_start(out=wr_bf[:], in_=wr.rearrange("(p t) -> p t", t=T4))
+        nc.scalar.dma_start(out=gain_bf[:], in_=edge_gain.rearrange("(p t) -> p t", t=T4))
 
         w1s = keep.tile([P, GROUPS, 1024], U8, name="w1s", align_bytes=64)
         w2s = keep.tile([P, CHAN], U8, name="w2s", align_bytes=64)
-        nc.gpsimd.memset(w1s[:].rearrange("p g n -> p (g n)").bitcast(I32), 0)
-        nc.gpsimd.memset(w2s[:].bitcast(I32), 0)
-        w1w = keep.tile([P, GROUPS, 2048], U8, name="w1w", align_bytes=64)
+        nc.vector.memset(w1s[:].rearrange("p g n -> p (g n)").bitcast(I32), 0)
+        nc.vector.memset(w2s[:].bitcast(I32), 0)
+        w1w = big([P, GROUPS, 2048], U8, "w1w")
         w2w = keep.tile([P, 1024], U8, name="w2w", align_bytes=64)
         w1s_dst = w1s[:].rearrange("p g n -> p (g n)").bitcast(I32).rearrange("p (g n) -> p g n", g=GROUPS)
         for q in range(4):
@@ -61,19 +76,10 @@ def tile_egnngatededgelayer_d1p_kernel(
                 out=w1s_dst[32 * q : 32 * q + 4],
                 in_=w1_scales.bitcast(I32)[:, 4 * q : 4 * q + 4, :].rearrange("g r n -> r g n"),
             )
-        posb = keep.tile([P, GRAPHS * NODES * 3], BF16, name="posb")
-        posj = keep.tile([P, GRAPHS, 4], BF16, name="posj")
-        nc.gpsimd.dma_start(out=posb[:], in_=pos.rearrange("b n c -> (b n c)").partition_broadcast(P))
-        for half in range(2):
-            nc.gpsimd.dma_start(out=posj[64 * half : 64 * half + 64, :, 0:3], in_=pos.rearrange("b j c -> j b c"))
         for g in range(GROUPS):
-            nc.sync.dma_start(
-                out=w1w[:, g, :].bitcast(I32), in_=w1_words[g].bitcast(I32)
-            )
-        wr_bf = keep.tile([P, T4], BF16, name="wr_bf")
-        gain_bf = keep.tile([P, T4], BF16, name="gain_bf")
-        nc.gpsimd.dma_start(out=wr_bf[:], in_=wr.rearrange("(p t) -> p t", t=T4))
-        nc.gpsimd.dma_start(out=gain_bf[:], in_=edge_gain.rearrange("(p t) -> p t", t=T4))
+            nc.sync.dma_start(out=w1w[:, g, :].bitcast(I32), in_=w1_words[g].bitcast(I32))
+        wrb = keep.tile([P, FEAT], BF16, name="wrb")
+        nc.sync.dma_start(out=wrb[:], in_=wr.partition_broadcast(P))
         nc.sync.dma_start(out=w2w[:].bitcast(I32), in_=w2_words[0].bitcast(I32))
         for q in range(4):
             nc.sync.dma_start(
@@ -86,29 +92,16 @@ def tile_egnngatededgelayer_d1p_kernel(
         warm = keep.tile([P, 1], F32, name="warm")
         nc.vector.memset(warm[:], 0.0)
         nc.scalar.activation(warm[:], warm[:], ACT.Silu)
-        ident = keep.tile([P, P], F32, name="ident")
-        make_identity(nc, ident[:])
-        ident_bf = keep.tile([P, P], BF16, name="ident_bf")
-        nc.gpsimd.tensor_copy(ident_bf[:], ident[:])
-        first_row = keep.tile([P, P], BF16, name="first_row")
-        nc.vector.memset(first_row[:], 0.0)
-        nc.vector.memset(first_row[0:1, :], 1.0)
-        consts = psum.tile([P, 1024], BF16, name="consts", tag="consts", bufs=1)
-        gw_ps = consts[:, 0:CHAN]
-        gain_ps = consts[:, CHAN : CHAN + T4]
 
-        hbf = [keep.tile([P, DEPTH], BF16, name=f"hbf{r}") for r in range(2)]
-        for r in range(2):
-            for kb in range(16):
-                cols = slice(kb * 128, kb * 128 + 128)
-                if kb % 2 == 0:
-                    nc.vector.tensor_scalar(
-                        hbf[r][:, cols], hb[r][:, cols].bitcast(FP8), hs[:, r, kb : kb + 1], None, ALU.mult
-                    )
-                else:
-                    nc.scalar.activation(
-                        hbf[r][:, cols], hb[r][:, cols].bitcast(FP8), ACT.Copy, scale=hs[:, r, kb : kb + 1]
-                    )
+        select = keep.tile([P, 8, 512], F32, name="select")
+        nc.vector.tensor_copy(
+            select[0:64].rearrange("p a (b i) -> p (a b) i", i=NODES),
+            ident[0:64, 0:64].unsqueeze(1).to_broadcast([64, 64, NODES]),
+        )
+        nc.vector.tensor_copy(
+            select[64:P].rearrange("p a (b i) -> p (a b) i", i=NODES),
+            ident[64:P, 64:P].unsqueeze(2).to_broadcast([64, 64, NODES]),
+        )
 
         wr_f = keep.tile([P, T4], F32, name="wr_f")
         nc.vector.tensor_copy(wr_f[:], wr_bf[:])
@@ -126,19 +119,49 @@ def tile_egnngatededgelayer_d1p_kernel(
         nc.vector.tensor_tensor(diff[:], diff[:], diff[:], ALU.mult)
         r2 = keep.tile([P, TILES], F32, name="r2")
         nc.vector.tensor_reduce(r2[:], diff[:], AX.X, ALU.add)
+        rt_ps = bank("pp", 2)
+        nc.tensor.transpose(rt_ps[:, 0:P], r2[:], ident[:])
 
-        hcodes = keep.tile([P, GROUPS, ROWS], U32, name="hcodes", align_bytes=64)
-        hplane = keep.tile([P, GROUPS, ROWS], U8, name="hplane", align_bytes=64)
-        hq = keep.tile([P, GROUPS, ROWS * 4], BF16, name="hq", align_bytes=64)
+        hbf = big([P, 2, DEPTH], BF16, "hbf")
+        for kb in range(16):
+            cols = slice(kb * 128, kb * 128 + 128)
+            for r in range(2):
+                if (2 * kb + r) % 8 in (0, 3, 6):
+                    nc.vector.tensor_scalar(
+                        hbf[:, r, cols], hb[r][:, cols].bitcast(FP8), hs[:, r, kb : kb + 1], None, ALU.mult
+                    )
+                else:
+                    nc.scalar.activation(
+                        hbf[:, r, cols], hb[r][:, cols].bitcast(FP8), ACT.Copy, scale=hs[:, r, kb : kb + 1]
+                    )
+        rT = keep.tile([P, P], F32, name="rT")
+        nc.scalar.copy(rT[:], rt_ps[:, 0:P])
+        flat = out.rearrange("b n c -> (b n c)")
+        nc.sync.dma_start(out=flat[0 : P * P].rearrange("(p f) -> p f", f=P), in_=rT[:])
+
+        def load_r2_row(b):
+            part = 96 + b % 2
+            nc.sync.dma_start(
+                out=select[part : part + 1, :, :].rearrange("p a e -> p (a e)"),
+                in_=flat[b * 4096 : (b + 1) * 4096].unsqueeze(0),
+            )
+
+        load_r2_row(0)
+        load_r2_row(1)
+
+        hcodes = keep.tile([P, GROUPS, ROWS + 64], U32, name="hcodes", align_bytes=64)
+        hplane = keep.tile([P, GROUPS, ROWS + 64], U8, name="hplane", align_bytes=64)
+        hq = big([P, GROUPS, ROWS * 4], BF16, "hq")
         xts = []
+        words = hbf[:].rearrange("p r k -> p (r k)").bitcast(F32)
         for g in range(GROUPS):
             xt = bank("mx", 4)
             xts.append(xt)
             xv = xt[:].rearrange("p (r u x) -> p r u x", r=2, u=2)
             for r in range(2):
-                words = hbf[r][:].bitcast(F32)
                 for u in range(2):
-                    nc.tensor.transpose(xv[:, r, u, :], words[:, 256 * g + u : 256 * (g + 1) : 2], ident[:])
+                    w0 = r * (DEPTH // 2) + 256 * g + u
+                    nc.tensor.transpose(xv[:, r, u, :], words[:, w0 : w0 + 256 - u : 2], ident[:])
         for g in range(GROUPS):
             dst = hq[:, g, :].bitcast(F32).rearrange("p (r x u) -> p r x u", r=2, u=2)
             src = xts[g][:].rearrange("p (r u x) -> p r x u", r=2, u=2)
@@ -147,45 +170,83 @@ def tile_egnngatededgelayer_d1p_kernel(
             else:
                 nc.scalar.copy(dst, src)
         for g in range(GROUPS):
-            nc.vector.quantize_mx(out=hcodes[:, g, :].bitcast(FP8X4), scales=hplane[:, g, :], in_=hq[:, g, :])
-        uv = [[bank("mx", 4) for half in range(2)] for r in range(2)]
-        for g in range(GROUPS):
-            for r in range(2):
-                for half in range(2):
-                    nc.tensor.matmul_mx(
-                        out=uv[r][half][:],
-                        lhsT=hcodes[:, g, r * P : (r + 1) * P].bitcast(FP8X4),
-                        lhsT_scale=hplane[:, g, r * P : (r + 1) * P],
-                        rhs=w1w[:, g, half * 1024 : (half + 1) * 1024].bitcast(FP4X4),
-                        rhs_scale=w1s[:, g, half * 512 : (half + 1) * 512],
-                        start=(g == 0),
-                        stop=(g == GROUPS - 1),
-                    )
+            nc.vector.quantize_mx(out=hcodes[:, g, 0:ROWS].bitcast(FP8X4), scales=hplane[:, g, 0:ROWS], in_=hq[:, g, :])
+        nc.vector.tensor_copy(hcodes[:, :, ROWS : ROWS + 64].bitcast(I32), hcodes[:, :, 0:64].bitcast(I32))
+        nc.vector.tensor_copy(hplane[:, :, ROWS : ROWS + 64], hplane[:, :, 0:64])
+
+        def first_product(ps, c0, half):
+            for g in range(GROUPS):
+                nc.tensor.matmul_mx(
+                    out=ps[:],
+                    lhsT=hcodes[:, g, c0 : c0 + P].bitcast(FP8X4),
+                    lhsT_scale=hplane[:, g, c0 : c0 + P],
+                    rhs=w1w[:, g, half * 1024 : (half + 1) * 1024].bitcast(FP4X4),
+                    rhs_scale=w1s[:, g, half * 512 : (half + 1) * 512],
+                    start=(g == 0),
+                    stop=(g == GROUPS - 1),
+                )
+
+        windows = [(0, 0), (64, 1), (128, 0), (192, 1)]
+        uv = [bank("mx", 4) for w in range(4)]
+        for w in (0, 3, 1, 2):
+            first_product(uv[w], windows[w][0], windows[w][1])
+
         uT = keep.tile([P, T4, ROWS], F32, name="uT")
         vT = keep.tile([P, T4, ROWS], F32, name="vT")
-        uvrow = keep.tile([P, 2, 2, T4, P], F32, name="uvrow")
-        for r in range(2):
-            for half in range(2):
-                src = uv[r][half][:].rearrange("p (m t) -> p t m", t=T4)
-                if half == 0:
-                    nc.vector.tensor_copy(uvrow[:, r, half], src)
-                else:
-                    nc.scalar.copy(uvrow[:, r, half], src)
-        for r in range(2):
-            for half in range(2):
-                tp = bank("mx", 4)
-                for t in range(T4):
-                    nc.tensor.transpose(tp[:, t * P : (t + 1) * P], uvrow[:, r, half, t, :], ident[:])
-                src = tp[:].rearrange("p (t x) -> p t x", t=T4)
-                if half == 0:
-                    nc.scalar.copy(uT[:, :, r * P : (r + 1) * P], src)
-                else:
-                    nc.vector.tensor_copy(vT[:, :, r * P : (r + 1) * P], src)
+        uvrow = big([P, 4, T4, P], F32, "uvrow")
+        for w in (0, 3, 1, 2):
+            src = uv[w][:].rearrange("p (m t) -> p t m", t=T4)
+            if w in (0, 1):
+                nc.vector.tensor_copy(uvrow[:, w], src)
+            else:
+                nc.scalar.copy(uvrow[:, w], src)
+        for w in (0, 3, 1, 2):
+            tp = bank("mx", 4)
+            for t in range(T4):
+                nc.tensor.transpose(tp[:, t * P : (t + 1) * P], uvrow[:, w, t, :], ident[:])
+            src = tp[:].rearrange("p (t x) -> p t x", t=T4)
+            if w == 0:
+                nc.vector.tensor_copy(uT[:, :, 0:P], src)
+            elif w == 3:
+                nc.scalar.copy(vT[:, :, 0:64], src[:, :, 64:P])
+                nc.scalar.copy(vT[:, :, 192:256], src[:, :, 0:64])
+            elif w == 1:
+                nc.scalar.copy(vT[:, :, 64 : 64 + P], src)
+            else:
+                nc.vector.tensor_copy(uT[:, :, P : 2 * P], src)
 
-        nc.tensor.matmul(gw_ps, lhsT=first_row[:], rhs=gw[:], start=True, stop=True)
-        nc.tensor.matmul(gain_ps, lhsT=ident_bf[:], rhs=gain_bf[:], start=True, stop=True)
+        lhs = [keep.tile([P, 2, P], F32, name=f"lhs{b}") for b in range(GRAPHS)]
+        wr_rows = wrb[96:98].rearrange("p (m t) -> p t m", t=T4)[:, 0:2, :]
+
+        def gp_copy(dst, src):
+            nc.gpsimd.tensor_scalar(dst, src, 1.0, 0.0, ALU.mult, ALU.add)
+
+        def lhs_wr(b):
+            if b % 2 == 0:
+                nc.gpsimd.memset(lhs[b][96:98], 0.0)
+                gp_copy(lhs[b][96:97], wr_rows[0:1])
+            else:
+                gp_copy(lhs[b][96:98], wr_rows)
+                nc.gpsimd.memset(lhs[b][96:97], 0.0)
+
+        for b in (0, 2):
+            gp_copy(lhs[b][0:64], uvrow[0:64, b, 0:2, :])
+            gp_copy(lhs[b][64:P], uvrow[64:P, 3 - b, 0:2, :])
+            lhs_wr(b)
+
+        def lhs_odd(x):
+            b, half = ((1, 0), (1, 1), (3, 0), (3, 1))[x]
+            rows = slice(64, P) if half else slice(0, 64)
+            ps = bank("acc", 1)
+            first_product(ps, 64 * (b - half), half)
+            nc.scalar.copy(lhs[b][rows], ps[rows].rearrange("p (m t) -> p t m", t=T4)[:, 0:2, :])
+            if half:
+                lhs_wr(b)
 
         state = {}
+
+        def on_pe(k):
+            return 0 < k < BLOCKS and k % 8 != 4
 
         def spread_r2(k):
             ps = bank("r2", 1)
@@ -194,37 +255,51 @@ def tile_egnngatededgelayer_d1p_kernel(
                 nc.tensor.transpose(ps[:, q * P : (q + 1) * P], r2[:, c : c + 1].to_broadcast([P, P]), ident[:])
             state["r2", k] = ps
 
-        def pre(k):
+        def pre_pe(k):
+            if not on_pe(k):
+                return
             b = k // 8
-            w = work.tile([P, T4, 512], F32, name="w", tag="w")
+            for t in range(2):
+                ps = bank("pp", 2)
+                nc.tensor.matmul(ps[:], lhsT=lhs[b][:, t, :], rhs=select[:, k % 8, :], start=True, stop=True)
+                state["pp", k, t] = ps
+            if k % 8 == 7 and b < 2:
+                load_r2_row(b + 2)
+
+        def pre_v(k):
+            b = k // 8
+            s = work.tile([P, T4, 512], F32, name="s", tag="s")
             ps = state["r2", k]
-            for t in range(T4):
+            for t in range(2 if on_pe(k) else 0, T4):
                 nc.vector.scalar_tensor_tensor(
-                    w[:, t, :].rearrange("p (i j) -> p i j", j=NODES),
+                    s[:, t, :].rearrange("p (i j) -> p i j", j=NODES),
                     ps[:].rearrange("p (i j) -> p i j", j=NODES),
                     wr_f[:, t : t + 1],
                     uT[:, t, b * NODES : (b + 1) * NODES].unsqueeze(1).to_broadcast([P, 8, NODES]),
                     ALU.mult,
                     ALU.add,
                 )
-            state["w", k] = w
+            state["s", k] = s
 
-        def silu1(k):
-            w = state["w", k]
-            s = work.tile([P, T4, 512], F32, name="s", tag="s")
-            for t in range(T4):
+        def silu1_pe(k):
+            if on_pe(k):
+                for t in range(2):
+                    nc.scalar.activation(state["s", k][:, t, :], state["pp", k, t][:], ACT.Silu)
+
+        def silu1_v(k):
+            s = state["s", k]
+            for t in range(2 if on_pe(k) else 0, T4):
                 for i in range(8):
                     e = slice(i * NODES, (i + 1) * NODES)
                     node = k * 8 + i
-                    nc.scalar.activation(s[:, t, e], w[:, t, e], ACT.Silu, bias=vT[:, t, node : node + 1])
-            state["s", k] = s
+                    nc.scalar.activation(s[:, t, e], s[:, t, e], ACT.Silu, bias=vT[:, t, node : node + 1])
 
         def gain(k):
             a = work.tile([P, 2048], BF16, name="a", tag="a", align_bytes=64)
             nc.vector.tensor_tensor(
-                a[:].rearrange("p (e t) -> p e t", t=T4),
-                state["s", k][:].rearrange("p t e -> p e t"),
-                gain_ps.unsqueeze(1).to_broadcast([P, 512, T4]),
+                a[:].rearrange("p (c i t) -> p c t i", i=4, t=T4),
+                state["s", k][:].rearrange("p t (c i) -> p c t i", i=4),
+                gain_bf[:].unsqueeze(1).unsqueeze(3).to_broadcast([P, 128, T4, 4]),
                 ALU.mult,
             )
             state["a", k] = a
@@ -263,92 +338,123 @@ def tile_egnngatededgelayer_d1p_kernel(
             for q in range(4):
                 junk = work.tile([P, CHAN], F32, name="junk", tag="junk")
                 nc.vector.scalar_tensor_tensor(
-                    junk[:], state["m", k][:, q, :], 1.0, gw_ps, ALU.mult, ALU.mult, accum_out=dot[:, q : q + 1]
+                    junk[:], state["m", k][:, q, :], 1.0, gw[:], ALU.mult, ALU.mult, accum_out=dot[:, q : q + 1]
                 )
             state["dot", k] = dot
 
-        def gate_tanh(k):
+        def gate(k):
             th = work.tile([P, 4], F32, name="th", tag="th")
             nc.scalar.activation(th[:], state["dot", k][:], ACT.Tanh, scale=0.5)
-            state["th", k] = th
-
-        def weigh(k):
             g = work.tile([P, 4], F32, name="g", tag="g")
-            nc.gpsimd.tensor_scalar(g[:], state["th", k][:], 1.0, 0.0625, ALU.add, ALU.mult)
-            gm = work.tile([P, 4, CHAN], F32, name="gm", tag="gm", bufs=8)
-            for q in range(4):
-                nc.gpsimd.tensor_scalar(
-                    gm[:, q, :], state["m", k][:, q, :], g[:, q : q + 1], 0.0, ALU.mult, ALU.add
+            nc.gpsimd.tensor_scalar(g[:], th[:], 1.0, 0.0625, ALU.add, ALU.mult)
+            state["g", k] = g
+            state["gm", k] = big([P, 4, CHAN], F32, "gm")
+
+        def weigh_s(k, tiles):
+            for q in tiles:
+                nc.scalar.activation(
+                    state["gm", k][:, q, :], state["m", k][:, q, :], ACT.Copy, scale=state["g", k][:, q : q + 1]
                 )
-            state["gm", k] = gm
+
+        def weigh_v(k, tiles):
+            for q in tiles:
+                nc.vector.tensor_scalar(
+                    state["gm", k][:, q, :], state["m", k][:, q, :], state["g", k][:, q : q + 1], None, ALU.mult
+                )
+
+        groups = [(4 * n, 4) for n in range(7)] + [(28, 2), (30, 1), (31, 1)]
 
         def add_up(n, slices):
+            first, count = groups[n]
             if 0 in slices:
-                state["acc", n] = bank("acc", 2)
+                state["acc", n] = bank("acc", 1) if count == 4 else bank("mx", 4)
             acc = state["acc", n]
             for s in slices:
-                for x in range(16):
+                for x in range(4 * count):
                     nc.tensor.matmul(
                         acc[:, s * P : (s + 1) * P],
-                        lhsT=state["gm", 4 * n + x // 4][:, x % 4, s * P : (s + 1) * P],
+                        lhsT=state["gm", first + x // 4][:, x % 4, s * P : (s + 1) * P],
                         rhs=ident[:],
                         is_transpose=True,
                         start=(x == 0),
-                        stop=(x == 15),
+                        stop=(x == 4 * count - 1),
                     )
 
         def collect(n):
-            b = n // 2
-            if n % 2 == 0:
-                part = work.tile([P, 512], F32, name="part", tag="part")
+            first, count = groups[n]
+            b = first // 8
+            part = work.tile([P, 512], F32, name="part", tag="part")
+            if first % 8 == 0:
                 nc.vector.tensor_copy(part[:], state["acc", n][:])
-                state["part"] = part
+            else:
+                nc.vector.tensor_tensor(part[:], state["acc", n][:], state["part"][:], ALU.add)
+            state["part"] = part
+            if (first + count) % 8 != 0:
                 return
-            both = work.tile([P, 4, 2, NODES], F32, name="both", tag="both")
-            nc.vector.tensor_tensor(
-                both[:].rearrange("p s h i -> p (s h i)"), state["acc", n][:], state["part"][:], ALU.add
-            )
+            halves = part[:].rearrange("p (s h i) -> p s h i", s=4, h=2)
             if b % 2 == 0:
-                oT = work.tile([P, 4, 2, NODES], F32, name="oT", tag="oT")
+                oT = work.tile([P, 4, 2, NODES], F32, name="oT", tag="oT", bufs=1)
                 state["oT"] = oT
             oT = state["oT"]
-            nc.vector.tensor_tensor(oT[:, :, b % 2, :], both[:, :, 0, :], both[:, :, 1, :], ALU.add)
+            nc.vector.tensor_tensor(oT[:, :, b % 2, :], halves[:, :, 0, :], halves[:, :, 1, :], ALU.add)
             if b % 2 == 1:
                 ps = bank("r2", 1)
                 for s in range(4):
                     nc.tensor.transpose(
                         ps[:, s * P : (s + 1) * P], oT[:, s].rearrange("p b i -> p (b i)"), ident[:]
                     )
-                res = work.tile([P, CHAN], F32, name="res", tag="res")
+                res = work.tile([P, CHAN], F32, name="res", tag="res", bufs=1)
                 nc.scalar.copy(res[:], ps[:])
                 nc.sync.dma_start(out=out.flatten_outer_dims()[(b // 2) * P : (b // 2 + 1) * P, :], in_=res[:])
 
         spread_r2(0)
-        pre(0)
-        silu1(0)
+        pre_v(0)
+        silu1_v(0)
         spread_r2(1)
-        for k in range(BLOCKS + 5):
+        pre_pe(1)
+        for k in range(BLOCKS):
             if k + 1 < BLOCKS:
-                pre(k + 1)
-            if 2 <= k < BLOCKS + 2:
-                weigh(k - 2)
-            if k % 4 == 2 and k >= 6:
-                add_up(k // 4 - 1, (0, 1))
-            if k % 4 == 3 and k >= 6:
-                add_up(k // 4 - 1, (2, 3))
-            if 1 <= k <= BLOCKS:
-                silu2(k - 1)
+                pre_v(k + 1)
+            if 2 <= k:
+                gate(k - 2)
             if k + 1 < BLOCKS:
-                silu1(k + 1)
+                silu1_pe(k + 1)
+            pre_pe(k + 2)
             if k + 2 < BLOCKS:
                 spread_r2(k + 2)
-            if k < BLOCKS:
-                gain(k)
-            if 1 <= k <= BLOCKS:
+            if 2 <= k:
+                weigh_s(k - 2, (0, 1, 2))
+            if 1 <= k:
+                silu2(k - 1)
+            if k + 1 < BLOCKS:
+                silu1_v(k + 1)
+            if 1 <= k <= 4:
+                lhs_odd(k - 1)
+            gain(k)
+            if 2 <= k:
+                weigh_v(k - 2, (3,))
+            quant(k)
+            product(k)
+            if k % 4 == 2 and k >= 10:
+                collect((k - 10) // 4)
+            if 6 <= k < 30:
+                add_up((k - 6) // 4, ((k - 6) % 4,))
+            elif k >= 30:
+                add_up(6, (0, 1) if k == 30 else (2, 3))
+            if 1 <= k:
                 gate_dot(k - 1)
-                gate_tanh(k - 1)
-            if k % 4 == 0 and k >= 8:
-                collect(k // 4 - 2)
-            if k < BLOCKS:
-                quant(k)
-                product(k)
+        gate(30)
+        weigh_s(30, (0, 1))
+        silu2(31)
+        weigh_v(30, (2, 3))
+        add_up(7, (0, 1, 2, 3))
+        collect(6)
+        gate_dot(31)
+        add_up(8, (0, 1, 2, 3))
+        gate(31)
+        collect(7)
+        weigh_s(31, (0, 1))
+        weigh_v(31, (2, 3))
+        collect(8)
+        add_up(9, (0, 1, 2, 3))
+        collect(9)

@@ -93,6 +93,15 @@ def tile_egnngatededgelayer_d1p_kernel(
         nc.vector.memset(warm[:], 0.0)
         nc.scalar.activation(warm[:], warm[:], ACT.Silu)
 
+        ident_bf = keep.tile([P, P], BF16, name="ident_bf")
+        nc.vector.tensor_copy(ident_bf[:], ident[:])
+        first_row = keep.tile([P, P], BF16, name="first_row")
+        nc.vector.memset(first_row[:], 0.0)
+        nc.vector.memset(first_row[0:1, :], 1.0)
+        consts = psum.tile([P, 1024], BF16, name="consts", tag="consts", bufs=1)
+        gw_ps = consts[:, 0:CHAN]
+        gain_ps = consts[:, CHAN : CHAN + T4]
+
         select = keep.tile([P, 8, 512], F32, name="select")
         nc.vector.tensor_copy(
             select[0:64].rearrange("p a (b i) -> p (a b) i", i=NODES),
@@ -119,7 +128,7 @@ def tile_egnngatededgelayer_d1p_kernel(
         nc.vector.tensor_tensor(diff[:], diff[:], diff[:], ALU.mult)
         r2 = keep.tile([P, TILES], F32, name="r2")
         nc.vector.tensor_reduce(r2[:], diff[:], AX.X, ALU.add)
-        rt_ps = bank("pp", 2)
+        rt_ps = bank("pp", 1)
         nc.tensor.transpose(rt_ps[:, 0:P], r2[:], ident[:])
 
         hbf = big([P, 2, DEPTH], BF16, "hbf")
@@ -243,6 +252,9 @@ def tile_egnngatededgelayer_d1p_kernel(
             if half:
                 lhs_wr(b)
 
+        nc.tensor.matmul(gw_ps, lhsT=first_row[:], rhs=gw[:], start=True, stop=True)
+        nc.tensor.matmul(gain_ps, lhsT=ident_bf[:], rhs=gain_bf[:], start=True, stop=True)
+
         state = {}
 
         def on_pe(k):
@@ -255,15 +267,14 @@ def tile_egnngatededgelayer_d1p_kernel(
                 nc.tensor.transpose(ps[:, q * P : (q + 1) * P], r2[:, c : c + 1].to_broadcast([P, P]), ident[:])
             state["r2", k] = ps
 
-        def pre_pe(k):
+        def pre_pe(k, t):
             if not on_pe(k):
                 return
             b = k // 8
-            for t in range(2):
-                ps = bank("pp", 2)
-                nc.tensor.matmul(ps[:], lhsT=lhs[b][:, t, :], rhs=select[:, k % 8, :], start=True, stop=True)
-                state["pp", k, t] = ps
-            if k % 8 == 7 and b < 2:
+            ps = bank("pp", 1)
+            nc.tensor.matmul(ps[:], lhsT=lhs[b][:, t, :], rhs=select[:, k % 8, :], start=True, stop=True)
+            state["pp", k, t] = ps
+            if k % 8 == 7 and t == 1 and b < 2:
                 load_r2_row(b + 2)
 
         def pre_v(k):
@@ -281,10 +292,9 @@ def tile_egnngatededgelayer_d1p_kernel(
                 )
             state["s", k] = s
 
-        def silu1_pe(k):
+        def silu1_pe(k, t):
             if on_pe(k):
-                for t in range(2):
-                    nc.scalar.activation(state["s", k][:, t, :], state["pp", k, t][:], ACT.Silu)
+                nc.scalar.activation(state["s", k][:, t, :], state["pp", k, t][:], ACT.Silu)
 
         def silu1_v(k):
             s = state["s", k]
@@ -299,7 +309,7 @@ def tile_egnngatededgelayer_d1p_kernel(
             nc.vector.tensor_tensor(
                 a[:].rearrange("p (c i t) -> p c t i", i=4, t=T4),
                 state["s", k][:].rearrange("p t (c i) -> p c t i", i=4),
-                gain_bf[:].unsqueeze(1).unsqueeze(3).to_broadcast([P, 128, T4, 4]),
+                gain_ps.unsqueeze(1).unsqueeze(3).to_broadcast([P, 128, T4, 4]),
                 ALU.mult,
             )
             state["a", k] = a
@@ -333,14 +343,27 @@ def tile_egnngatededgelayer_d1p_kernel(
                 nc.scalar.activation(m[:, q, :], state["mx", k][q][:], ACT.Silu)
             state["m", k] = m
 
-        def gate_dot(k):
-            dot = work.tile([P, 4], F32, name="dot", tag="dot")
-            for q in range(4):
+        def gate_dot(k, tiles):
+            if 0 in tiles:
+                dot = work.tile([P, 4], F32, name="dot", tag="dot")
+                state["dot", k] = dot
+            dot = state["dot", k]
+            for q in tiles:
                 junk = work.tile([P, CHAN], F32, name="junk", tag="junk")
                 nc.vector.scalar_tensor_tensor(
-                    junk[:], state["m", k][:, q, :], 1.0, gw[:], ALU.mult, ALU.mult, accum_out=dot[:, q : q + 1]
+                    junk[:], state["m", k][:, q, :], 1.0, gw_ps, ALU.mult, ALU.mult, accum_out=dot[:, q : q + 1]
                 )
-            state["dot", k] = dot
+
+        def gate_dot_g(k, q):
+            prod = work.tile([P, CHAN], F32, name="prod", tag="prod")
+            nc.gpsimd.tensor_tensor(prod[:], state["m", k][:, q, :], gw[:], ALU.mult)
+            state["prod", k] = prod
+
+        def gate_dot_s(k, q):
+            junk_s = work.tile([P, CHAN], F32, name="junk_s", tag="junk_s", bufs=1)
+            nc.scalar.activation(
+                junk_s[:], state["prod", k][:], ACT.Copy, accum_out=state["dot", k][:, q : q + 1]
+            )
 
         def gate(k):
             th = work.tile([P, 4], F32, name="th", tag="th")
@@ -354,6 +377,12 @@ def tile_egnngatededgelayer_d1p_kernel(
             for q in tiles:
                 nc.scalar.activation(
                     state["gm", k][:, q, :], state["m", k][:, q, :], ACT.Copy, scale=state["g", k][:, q : q + 1]
+                )
+
+        def weigh_g(k, tiles):
+            for q in tiles:
+                nc.gpsimd.tensor_scalar(
+                    state["gm", k][:, q, :], state["m", k][:, q, :], state["g", k][:, q : q + 1], 0.0, ALU.mult, ALU.add
                 )
 
         def weigh_v(k, tiles):
@@ -411,45 +440,50 @@ def tile_egnngatededgelayer_d1p_kernel(
         pre_v(0)
         silu1_v(0)
         spread_r2(1)
-        pre_pe(1)
+        pre_pe(1, 0)
         for k in range(BLOCKS):
             if k + 1 < BLOCKS:
                 pre_v(k + 1)
             if 2 <= k:
                 gate(k - 2)
+                weigh_g(k - 2, (0, 1, 2))
             if k + 1 < BLOCKS:
-                silu1_pe(k + 1)
-            pre_pe(k + 2)
-            if k + 2 < BLOCKS:
-                spread_r2(k + 2)
-            if 2 <= k:
-                weigh_s(k - 2, (0, 1, 2))
+                silu1_pe(k + 1, 0)
+                pre_pe(k + 1, 1)
             if 1 <= k:
                 silu2(k - 1)
+                gate_dot_g(k - 1, 3)
             if k + 1 < BLOCKS:
+                silu1_pe(k + 1, 1)
                 silu1_v(k + 1)
+            if 2 <= k:
+                weigh_s(k - 2, (3,))
+            if k + 2 < BLOCKS:
+                spread_r2(k + 2)
             if 1 <= k <= 4:
                 lhs_odd(k - 1)
-            gain(k)
-            if 2 <= k:
-                weigh_v(k - 2, (3,))
-            quant(k)
-            product(k)
             if k % 4 == 2 and k >= 10:
                 collect((k - 10) // 4)
             if 6 <= k < 30:
                 add_up((k - 6) // 4, ((k - 6) % 4,))
             elif k >= 30:
                 add_up(6, (0, 1) if k == 30 else (2, 3))
+            pre_pe(k + 2, 0)
+            gain(k)
             if 1 <= k:
-                gate_dot(k - 1)
+                gate_dot(k - 1, (0,))
+            quant(k)
+            product(k)
+            if 1 <= k:
+                gate_dot(k - 1, (1, 2))
+                gate_dot_s(k - 1, 3)
         gate(30)
         weigh_s(30, (0, 1))
         silu2(31)
         weigh_v(30, (2, 3))
         add_up(7, (0, 1, 2, 3))
         collect(6)
-        gate_dot(31)
+        gate_dot(31, (0, 1, 2, 3))
         add_up(8, (0, 1, 2, 3))
         gate(31)
         collect(7)

@@ -107,11 +107,19 @@ def tile_egnngatededgelayer_d1p_kernel(
             select[0:64].rearrange("p a (b i) -> p (a b) i", i=NODES),
             ident[0:64, 0:64].unsqueeze(1).to_broadcast([64, 64, NODES]),
         )
-        nc.vector.tensor_copy(
-            select[64:P].rearrange("p a (b i) -> p (a b) i", i=NODES),
-            ident[64:P, 64:P].unsqueeze(2).to_broadcast([64, 64, NODES]),
-        )
 
+        hbf = big([P, 2, DEPTH], BF16, "hbf")
+        for kb in range(16):
+            cols = slice(kb * 128, kb * 128 + 128)
+            for r in range(2):
+                if (2 * kb + r) % 8 in (0, 3, 6):
+                    nc.vector.tensor_scalar(
+                        hbf[:, r, cols], hb[r][:, cols].bitcast(FP8), hs[:, r, kb : kb + 1], None, ALU.mult
+                    )
+                else:
+                    nc.scalar.activation(
+                        hbf[:, r, cols], hb[r][:, cols].bitcast(FP8), ACT.Copy, scale=hs[:, r, kb : kb + 1]
+                    )
         wr_f = keep.tile([P, T4], F32, name="wr_f")
         nc.vector.tensor_copy(wr_f[:], wr_bf[:])
         diff = keep.tile([P, TILES, 3], F32, name="diff")
@@ -128,21 +136,13 @@ def tile_egnngatededgelayer_d1p_kernel(
         nc.vector.tensor_tensor(diff[:], diff[:], diff[:], ALU.mult)
         r2 = keep.tile([P, TILES], F32, name="r2")
         nc.vector.tensor_reduce(r2[:], diff[:], AX.X, ALU.add)
-        rt_ps = bank("pp", 1)
+        rt_ps = bank("pp", 2)
         nc.tensor.transpose(rt_ps[:, 0:P], r2[:], ident[:])
 
-        hbf = big([P, 2, DEPTH], BF16, "hbf")
-        for kb in range(16):
-            cols = slice(kb * 128, kb * 128 + 128)
-            for r in range(2):
-                if (2 * kb + r) % 8 in (0, 3, 6):
-                    nc.vector.tensor_scalar(
-                        hbf[:, r, cols], hb[r][:, cols].bitcast(FP8), hs[:, r, kb : kb + 1], None, ALU.mult
-                    )
-                else:
-                    nc.scalar.activation(
-                        hbf[:, r, cols], hb[r][:, cols].bitcast(FP8), ACT.Copy, scale=hs[:, r, kb : kb + 1]
-                    )
+        nc.vector.tensor_copy(
+            select[64:P].rearrange("p a (b i) -> p (a b) i", i=NODES),
+            ident[64:P, 64:P].unsqueeze(2).to_broadcast([64, 64, NODES]),
+        )
         rT = keep.tile([P, P], F32, name="rT")
         nc.scalar.copy(rT[:], rt_ps[:, 0:P])
         flat = out.rearrange("b n c -> (b n c)")
@@ -164,7 +164,7 @@ def tile_egnngatededgelayer_d1p_kernel(
         xts = []
         words = hbf[:].rearrange("p r k -> p (r k)").bitcast(F32)
         for g in range(GROUPS):
-            xt = bank("mx", 4)
+            xt = bank("mx", 3) if g < 3 else bank("acc", 1)
             xts.append(xt)
             xv = xt[:].rearrange("p (r u x) -> p r u x", r=2, u=2)
             for r in range(2):
@@ -179,26 +179,29 @@ def tile_egnngatededgelayer_d1p_kernel(
             else:
                 nc.scalar.copy(dst, src)
         for g in range(GROUPS):
-            nc.vector.quantize_mx(out=hcodes[:, g, 0:ROWS].bitcast(FP8X4), scales=hplane[:, g, 0:ROWS], in_=hq[:, g, :])
-        nc.vector.tensor_copy(hcodes[:, :, ROWS : ROWS + 64].bitcast(I32), hcodes[:, :, 0:64].bitcast(I32))
-        nc.vector.tensor_copy(hplane[:, :, ROWS : ROWS + 64], hplane[:, :, 0:64])
-
-        def first_product(ps, c0, half):
-            for g in range(GROUPS):
-                nc.tensor.matmul_mx(
-                    out=ps[:],
-                    lhsT=hcodes[:, g, c0 : c0 + P].bitcast(FP8X4),
-                    lhsT_scale=hplane[:, g, c0 : c0 + P],
-                    rhs=w1w[:, g, half * 1024 : (half + 1) * 1024].bitcast(FP4X4),
-                    rhs_scale=w1s[:, g, half * 512 : (half + 1) * 512],
-                    start=(g == 0),
-                    stop=(g == GROUPS - 1),
+            for dst, cols in (((0, ROWS), (0, ROWS * 4)), ((ROWS, ROWS + 64), (0, 256))):
+                nc.vector.quantize_mx(
+                    out=hcodes[:, g, dst[0] : dst[1]].bitcast(FP8X4),
+                    scales=hplane[:, g, dst[0] : dst[1]],
+                    in_=hq[:, g, cols[0] : cols[1]],
                 )
 
+        def first_product(ps, g, c0, half):
+            nc.tensor.matmul_mx(
+                out=ps[:],
+                lhsT=hcodes[:, g, c0 : c0 + P].bitcast(FP8X4),
+                lhsT_scale=hplane[:, g, c0 : c0 + P],
+                rhs=w1w[:, g, half * 1024 : (half + 1) * 1024].bitcast(FP4X4),
+                rhs_scale=w1s[:, g, half * 512 : (half + 1) * 512],
+                start=(g == 0),
+                stop=(g == GROUPS - 1),
+            )
+
         windows = [(0, 0), (64, 1), (128, 0), (192, 1)]
-        uv = [bank("mx", 4) for w in range(4)]
-        for w in (0, 3, 1, 2):
-            first_product(uv[w], windows[w][0], windows[w][1])
+        uv = [bank("mx", 3), bank("mx", 3), bank("acc", 1), bank("mx", 3)]
+        for g in range(GROUPS):
+            for w in (0, 3, 1, 2):
+                first_product(uv[w], g, windows[w][0], windows[w][1])
 
         uT = keep.tile([P, T4, ROWS], F32, name="uT")
         vT = keep.tile([P, T4, ROWS], F32, name="vT")
@@ -210,7 +213,7 @@ def tile_egnngatededgelayer_d1p_kernel(
             else:
                 nc.scalar.copy(uvrow[:, w], src)
         for w in (0, 3, 1, 2):
-            tp = bank("mx", 4)
+            tp = bank("mx", 3)
             for t in range(T4):
                 nc.tensor.transpose(tp[:, t * P : (t + 1) * P], uvrow[:, w, t, :], ident[:])
             src = tp[:].rearrange("p (t x) -> p t x", t=T4)
@@ -247,7 +250,8 @@ def tile_egnngatededgelayer_d1p_kernel(
             b, half = ((1, 0), (1, 1), (3, 0), (3, 1))[x]
             rows = slice(64, P) if half else slice(0, 64)
             ps = bank("acc", 1)
-            first_product(ps, 64 * (b - half), half)
+            for g in range(GROUPS):
+                first_product(ps, g, 64 * (b - half), half)
             nc.scalar.copy(lhs[b][rows], ps[rows].rearrange("p (m t) -> p t m", t=T4)[:, 0:2, :])
             if half:
                 lhs_wr(b)
@@ -271,7 +275,7 @@ def tile_egnngatededgelayer_d1p_kernel(
             if not on_pe(k):
                 return
             b = k // 8
-            ps = bank("pp", 1)
+            ps = bank("pp", 2)
             nc.tensor.matmul(ps[:], lhsT=lhs[b][:, t, :], rhs=select[:, k % 8, :], start=True, stop=True)
             state["pp", k, t] = ps
             if k % 8 == 7 and t == 1 and b < 2:
@@ -320,11 +324,10 @@ def tile_egnngatededgelayer_d1p_kernel(
             nc.vector.quantize_mx(out=codes[:].bitcast(FP8X4), scales=plane[:], in_=state["a", k][:])
             state["q", k] = (codes, plane)
 
-        def product(k):
+        def product(k, tiles):
             codes, plane = state["q", k]
-            banks = []
-            for q in range(4):
-                ps = bank("mx", 4)
+            for q in tiles:
+                ps = bank("mx", 3)
                 nc.tensor.matmul_mx(
                     out=ps[:],
                     lhsT=codes[:, q * P : (q + 1) * P].bitcast(FP8X4),
@@ -334,14 +337,15 @@ def tile_egnngatededgelayer_d1p_kernel(
                     start=True,
                     stop=True,
                 )
-                banks.append(ps)
-            state["mx", k] = banks
+                state["mx", k, q] = ps
 
-        def silu2(k):
-            m = work.tile([P, 4, CHAN], F32, name="m", tag="m", bufs=3)
-            for q in range(4):
-                nc.scalar.activation(m[:, q, :], state["mx", k][q][:], ACT.Silu)
-            state["m", k] = m
+        def silu2(k, tiles):
+            if 0 in tiles:
+                m = work.tile([P, 4, CHAN], F32, name="m", tag="m", bufs=3)
+                state["m", k] = m
+            m = state["m", k]
+            for q in tiles:
+                nc.scalar.activation(m[:, q, :], state["mx", k, q][:], ACT.Silu)
 
         def gate_dot(k, tiles):
             if 0 in tiles:
@@ -354,15 +358,18 @@ def tile_egnngatededgelayer_d1p_kernel(
                     junk[:], state["m", k][:, q, :], 1.0, gw_ps, ALU.mult, ALU.mult, accum_out=dot[:, q : q + 1]
                 )
 
+        def gp_tiles(k):
+            return (3,)
+
         def gate_dot_g(k, q):
-            prod = work.tile([P, CHAN], F32, name="prod", tag="prod")
+            prod = work.tile([P, CHAN], F32, name="prod", tag="prod", bufs=3)
             nc.gpsimd.tensor_tensor(prod[:], state["m", k][:, q, :], gw[:], ALU.mult)
-            state["prod", k] = prod
+            state["prod", k, q] = prod
 
         def gate_dot_s(k, q):
             junk_s = work.tile([P, CHAN], F32, name="junk_s", tag="junk_s", bufs=1)
             nc.scalar.activation(
-                junk_s[:], state["prod", k][:], ACT.Copy, accum_out=state["dot", k][:, q : q + 1]
+                junk_s[:], state["prod", k, q][:], ACT.Copy, accum_out=state["dot", k][:, q : q + 1]
             )
 
         def gate(k):
@@ -396,7 +403,7 @@ def tile_egnngatededgelayer_d1p_kernel(
         def add_up(n, slices):
             first, count = groups[n]
             if 0 in slices:
-                state["acc", n] = bank("acc", 1) if count == 4 else bank("mx", 4)
+                state["acc", n] = bank("acc", 1) if count == 4 else bank("mx", 3)
             acc = state["acc", n]
             for s in slices:
                 for x in range(4 * count):
@@ -441,25 +448,32 @@ def tile_egnngatededgelayer_d1p_kernel(
         silu1_v(0)
         spread_r2(1)
         pre_pe(1, 0)
+        pre_pe(1, 1)
         for k in range(BLOCKS):
-            if k + 1 < BLOCKS:
+            nxt = k + 1 < BLOCKS
+            if nxt:
                 pre_v(k + 1)
             if 2 <= k:
                 gate(k - 2)
                 weigh_g(k - 2, (0, 1, 2))
-            if k + 1 < BLOCKS:
-                silu1_pe(k + 1, 0)
-                pre_pe(k + 1, 1)
             if 1 <= k:
-                silu2(k - 1)
-                gate_dot_g(k - 1, 3)
-            if k + 1 < BLOCKS:
+                product(k - 1, (0, 1, 2))
+            if nxt:
+                silu1_pe(k + 1, 0)
                 silu1_pe(k + 1, 1)
+            pre_pe(k + 2, 0)
+            if 1 <= k:
+                silu2(k - 1, (0,))
+                product(k - 1, (3,))
+                silu2(k - 1, (1, 2, 3))
+                gate_dot_g(k - 1, 3)
+            pre_pe(k + 2, 1)
+            if k + 2 < BLOCKS:
+                spread_r2(k + 2)
+            if nxt:
                 silu1_v(k + 1)
             if 2 <= k:
                 weigh_s(k - 2, (3,))
-            if k + 2 < BLOCKS:
-                spread_r2(k + 2)
             if 1 <= k <= 4:
                 lhs_odd(k - 1)
             if k % 4 == 2 and k >= 10:
@@ -468,27 +482,27 @@ def tile_egnngatededgelayer_d1p_kernel(
                 add_up((k - 6) // 4, ((k - 6) % 4,))
             elif k >= 30:
                 add_up(6, (0, 1) if k == 30 else (2, 3))
-            pre_pe(k + 2, 0)
             gain(k)
             if 1 <= k:
                 gate_dot(k - 1, (0,))
             quant(k)
-            product(k)
             if 1 <= k:
                 gate_dot(k - 1, (1, 2))
                 gate_dot_s(k - 1, 3)
+        product(31, (0, 1, 2))
         gate(30)
-        weigh_s(30, (0, 1))
-        silu2(31)
-        weigh_v(30, (2, 3))
+        silu2(31, (0,))
+        product(31, (3,))
+        silu2(31, (1, 2, 3))
+        weigh_v(30, (0, 1, 2, 3))
         add_up(7, (0, 1, 2, 3))
         collect(6)
         gate_dot(31, (0, 1, 2, 3))
         add_up(8, (0, 1, 2, 3))
         gate(31)
         collect(7)
-        weigh_s(31, (0, 1))
-        weigh_v(31, (2, 3))
+        weigh_s(31, (0,))
+        weigh_v(31, (1, 2, 3))
         collect(8)
         add_up(9, (0, 1, 2, 3))
         collect(9)

from contextlib import ExitStack

import concourse.mybir as mybir
from concourse.masks import make_identity

F32 = mybir.dt.float32
BF16 = mybir.dt.bfloat16
U32 = mybir.dt.uint32
U8 = mybir.dt.uint8
I32 = mybir.dt.int32
FP8 = mybir.dt.float8_e4m3fn
FP8X4 = mybir.dt.float8_e4m3fn_x4
FP4X4 = mybir.dt.float4_e2m1fn_x4
ACT = mybir.ActivationFunctionType
ALU = mybir.AluOpType
AX = mybir.AxisListType

FLOPS = 2 * 256 * 2048 * 1024 + 2 * 16384 * 512 * 512

P = 128
GRAPHS, NODES, DEPTH, FEAT, CHAN = 4, 64, 2048, 512, 512
ROWS = GRAPHS * NODES
GROUPS = DEPTH // 512
T4 = 4
TILES = GRAPHS * NODES * NODES // P
PER_GRAPH = TILES // GRAPHS
BLOCKS = TILES // 4


def tile_egnngatededgelayer_d1p_kernel(
    tc, h_bytes, h_scale, pos, w1_words, w1_scales, wr, edge_gain, w2_words, w2_scales, gate_w, out
):
    nc = tc.nc
    with ExitStack() as ctx:
        keep = ctx.enter_context(tc.tile_pool(name="keep", bufs=1))
        work = ctx.enter_context(tc.tile_pool(name="work", bufs=2))
        psum = ctx.enter_context(tc.psum_pool(name="psum", bufs=2))
        ctx.enter_context(tc.manual_schedule())

        def big(shape, dtype, label):
            big_tile = work.tile(shape, dtype, name=label, tag="gm", bufs=9, align_bytes=64)
            return big_tile

        def bank(tag, bufs):
            ps_tile = psum.tile([P, 512], F32, name=tag, tag=tag, bufs=bufs)
            return ps_tile

        hb = [keep.tile([P, DEPTH], U8, name=f"hb{r}") for r in range(2)]
        hs = keep.tile([P, 2, 16], F32, name="hs")
        h_rows = h_bytes.flatten_outer_dims()
        nc.scalar.dma_start(out=hs[:], in_=h_scale.flatten_outer_dims().rearrange("(r p) k -> p r k", p=P))
        for r in range(2):
            nc.sync.dma_start(out=hb[r][:], in_=h_rows[r * P : (r + 1) * P, :])
        ident = keep.tile([P, P], F32, name="ident")
        make_identity(nc, ident[:])

        posb = keep.tile([P, GRAPHS * NODES * 3], BF16, name="posb")
        posj = keep.tile([P, GRAPHS, 4], BF16, name="posj")
        nc.scalar.dma_start(out=posb[:], in_=pos.rearrange("b n c -> (b n c)").partition_broadcast(P))
        for half in range(2):
            nc.scalar.dma_start(out=posj[64 * half : 64 * half + 64, :, 0:3], in_=pos.rearrange("b j c -> j b c"))
        wr_bf = keep.tile([P, T4], BF16, name="wr_bf")
        gain_bf = keep.tile([P, T4], BF16, name="gain_bf")
        nc.scalar.dma_start(out=wr_bf[:], in_=wr.rearrange("(p t) -> p t", t=T4))
        nc.scalar.dma_start(out=gain_bf[:], in_=edge_gain.rearrange("(p t) -> p t", t=T4))

        w1s = keep.tile([P, GROUPS, 1024], U8, name="w1s", align_bytes=64)
        w2s = keep.tile([P, CHAN], U8, name="w2s", align_bytes=64)
        nc.vector.memset(w1s[:].rearrange("p g n -> p (g n)").bitcast(I32), 0)
        nc.vector.memset(w2s[:].bitcast(I32), 0)
        w1w = big([P, GROUPS, 2048], U8, "w1w")
        w2w = keep.tile([P, 1024], U8, name="w2w", align_bytes=64)
        w1s_dst = w1s[:].rearrange("p g n -> p (g n)").bitcast(I32).rearrange("p (g n) -> p g n", g=GROUPS)
        for q in range(4):
            nc.sync.dma_start(
                out=w1s_dst[32 * q : 32 * q + 4],
                in_=w1_scales.bitcast(I32)[:, 4 * q : 4 * q + 4, :].rearrange("g r n -> r g n"),
            )
        for g in range(GROUPS):
            nc.sync.dma_start(out=w1w[:, g, :].bitcast(I32), in_=w1_words[g].bitcast(I32))
        wrb = keep.tile([P, FEAT], BF16, name="wrb")
        nc.sync.dma_start(out=wrb[:], in_=wr.partition_broadcast(P))
        nc.sync.dma_start(out=w2w[:].bitcast(I32), in_=w2_words[0].bitcast(I32))
        for q in range(4):
            nc.sync.dma_start(
                out=w2s[32 * q : 32 * q + 4, :].bitcast(I32),
                in_=w2_scales[0].bitcast(I32)[4 * q : 4 * q + 4, :],
            )
        gw = keep.tile([P, CHAN], BF16, name="gw")
        nc.sync.dma_start(out=gw[:], in_=gate_w.partition_broadcast(P))

        warm = keep.tile([P, 1], F32, name="warm")
        nc.vector.memset(warm[:], 0.0)
        nc.scalar.activation(warm[:], warm[:], ACT.Silu)

        ident_bf = keep.tile([P, P], BF16, name="ident_bf")
        nc.vector.tensor_copy(ident_bf[:], ident[:])
        first_row = keep.tile([P, P], BF16, name="first_row")
        nc.vector.memset(first_row[:], 0.0)
        nc.vector.memset(first_row[0:1, :], 1.0)
        consts = psum.tile([P, 1024], BF16, name="consts", tag="consts", bufs=1)
        gw_ps = consts[:, 0:CHAN]
        gain_ps = consts[:, CHAN : CHAN + T4]

        select = keep.tile([P, 8, 512], F32, name="select")
        nc.vector.tensor_copy(
            select[0:64].rearrange("p a (b i) -> p (a b) i", i=NODES),
            ident[0:64, 0:64].unsqueeze(1).to_broadcast([64, 64, NODES]),
        )

        hbf = big([P, 2, DEPTH], BF16, "hbf")
        for kb in range(16):
            cols = slice(kb * 128, kb * 128 + 128)
            for r in range(2):
                if (2 * kb + r) % 8 in (0, 3, 6):
                    nc.vector.tensor_scalar(
                        hbf[:, r, cols], hb[r][:, cols].bitcast(FP8), hs[:, r, kb : kb + 1], None, ALU.mult
                    )
                else:
                    nc.scalar.activation(
                        hbf[:, r, cols], hb[r][:, cols].bitcast(FP8), ACT.Copy, scale=hs[:, r, kb : kb + 1]
                    )
        wr_f = keep.tile([P, T4], F32, name="wr_f")
        nc.vector.tensor_copy(wr_f[:], wr_bf[:])
        diff = keep.tile([P, TILES, 3], F32, name="diff")
        posb_v = posb[:].rearrange("p (b s i c) -> p b s i c", b=GRAPHS, i=2, c=3)
        for b in range(GRAPHS):
            for half in range(2):
                rows = slice(64 * half, 64 * half + 64)
                nc.vector.tensor_tensor(
                    diff[rows, b * PER_GRAPH : (b + 1) * PER_GRAPH, :],
                    posb_v[rows, b, :, half, :],
                    posj[rows, b, 0:3].unsqueeze(1).to_broadcast([64, PER_GRAPH, 3]),
                    ALU.subtract,
                )
        nc.vector.tensor_tensor(diff[:], diff[:], diff[:], ALU.mult)
        r2 = keep.tile([P, TILES], F32, name="r2")
        nc.vector.tensor_reduce(r2[:], diff[:], AX.X, ALU.add)
        rt_ps = bank("pp", 2)
        nc.tensor.transpose(rt_ps[:, 0:P], r2[:], ident[:])

        nc.vector.tensor_copy(
            select[64:P].rearrange("p a (b i) -> p (a b) i", i=NODES),
            ident[64:P, 64:P].unsqueeze(2).to_broadcast([64, 64, NODES]),
        )
        rT = keep.tile([P, P], F32, name="rT")
        nc.scalar.copy(rT[:], rt_ps[:, 0:P])
        flat = out.rearrange("b n c -> (b n c)")
        nc.sync.dma_start(out=flat[0 : P * P].rearrange("(p f) -> p f", f=P), in_=rT[:])

        def load_r2_row(b):
            part = 96 + b % 2
            nc.sync.dma_start(
                out=select[part : part + 1, :, :].rearrange("p a e -> p (a e)"),
                in_=flat[b * 4096 : (b + 1) * 4096].unsqueeze(0),
            )

        load_r2_row(0)
        load_r2_row(1)

        hcodes = keep.tile([P, GROUPS, ROWS + 64], U32, name="hcodes", align_bytes=64)
        hplane = keep.tile([P, GROUPS, ROWS + 64], U8, name="hplane", align_bytes=64)
        hq = big([P, GROUPS, ROWS * 4], BF16, "hq")
        xts = []
        words = hbf[:].rearrange("p r k -> p (r k)").bitcast(F32)
        for g in range(GROUPS):
            xt = bank("mx", 3) if g < 3 else bank("acc", 1)
            xts.append(xt)
            xv = xt[:].rearrange("p (r u x) -> p r u x", r=2, u=2)
            for r in range(2):
                for u in range(2):
                    w0 = r * (DEPTH // 2) + 256 * g + u
                    nc.tensor.transpose(xv[:, r, u, :], words[:, w0 : w0 + 256 - u : 2], ident[:])
        for g in range(GROUPS):
            dst = hq[:, g, :].bitcast(F32).rearrange("p (r x u) -> p r x u", r=2, u=2)
            src = xts[g][:].rearrange("p (r u x) -> p r x u", r=2, u=2)
            if g % 2 == 0:
                nc.vector.tensor_copy(dst, src)
            else:
                nc.scalar.copy(dst, src)
        for g in range(GROUPS):
            for dst, cols in (((0, ROWS), (0, ROWS * 4)), ((ROWS, ROWS + 64), (0, 256))):
                nc.vector.quantize_mx(
                    out=hcodes[:, g, dst[0] : dst[1]].bitcast(FP8X4),
                    scales=hplane[:, g, dst[0] : dst[1]],
                    in_=hq[:, g, cols[0] : cols[1]],
                )

        def first_product(ps, g, c0, half):
            nc.tensor.matmul_mx(
                out=ps[:],
                lhsT=hcodes[:, g, c0 : c0 + P].bitcast(FP8X4),
                lhsT_scale=hplane[:, g, c0 : c0 + P],
                rhs=w1w[:, g, half * 1024 : (half + 1) * 1024].bitcast(FP4X4),
                rhs_scale=w1s[:, g, half * 512 : (half + 1) * 512],
                start=(g == 0),
                stop=(g == GROUPS - 1),
            )

        windows = [(0, 0), (64, 1), (128, 0), (192, 1)]
        uv = [bank("mx", 3), bank("mx", 3), bank("acc", 1), bank("mx", 3)]
        for g in range(GROUPS):
            for w in (0, 3, 1, 2):
                first_product(uv[w], g, windows[w][0], windows[w][1])

        uT = keep.tile([P, T4, ROWS], F32, name="uT")
        vT = keep.tile([P, T4, ROWS], F32, name="vT")
        uvrow = big([P, 4, T4, P], F32, "uvrow")
        for w in (0, 3, 1, 2):
            src = uv[w][:].rearrange("p (m t) -> p t m", t=T4)
            if w in (0, 1):
                nc.vector.tensor_copy(uvrow[:, w], src)
            else:
                nc.scalar.copy(uvrow[:, w], src)
        for w in (0, 3, 1, 2):
            tp = bank("mx", 3)
            for t in range(T4):
                nc.tensor.transpose(tp[:, t * P : (t + 1) * P], uvrow[:, w, t, :], ident[:])
            src = tp[:].rearrange("p (t x) -> p t x", t=T4)
            if w == 0:
                nc.vector.tensor_copy(uT[:, :, 0:P], src)
            elif w == 3:
                nc.scalar.copy(vT[:, :, 0:64], src[:, :, 64:P])
                nc.scalar.copy(vT[:, :, 192:256], src[:, :, 0:64])
            elif w == 1:
                nc.scalar.copy(vT[:, :, 64 : 64 + P], src)
            else:
                nc.vector.tensor_copy(uT[:, :, P : 2 * P], src)

        lhs = [keep.tile([P, 2, P], F32, name=f"lhs{b}") for b in range(GRAPHS)]
        wr_rows = wrb[96:98].rearrange("p (m t) -> p t m", t=T4)[:, 0:2, :]

        def gp_copy(dst, src):
            nc.gpsimd.tensor_scalar(dst, src, 1.0, 0.0, ALU.mult, ALU.add)

        def lhs_wr(b):
            if b % 2 == 0:
                nc.gpsimd.memset(lhs[b][96:98], 0.0)
                gp_copy(lhs[b][96:97], wr_rows[0:1])
            else:
                gp_copy(lhs[b][96:98], wr_rows)
                nc.gpsimd.memset(lhs[b][96:97], 0.0)

        for b in (0, 2):
            gp_copy(lhs[b][0:64], uvrow[0:64, b, 0:2, :])
            gp_copy(lhs[b][64:P], uvrow[64:P, 3 - b, 0:2, :])
            lhs_wr(b)

        def lhs_odd(x):
            b, half = ((1, 0), (1, 1), (3, 0), (3, 1))[x]
            rows = slice(64, P) if half else slice(0, 64)
            ps = bank("acc", 1)
            for g in range(GROUPS):
                first_product(ps, g, 64 * (b - half), half)
            nc.scalar.copy(lhs[b][rows], ps[rows].rearrange("p (m t) -> p t m", t=T4)[:, 0:2, :])
            if half:
                lhs_wr(b)

        nc.tensor.matmul(gw_ps, lhsT=first_row[:], rhs=gw[:], start=True, stop=True)
        nc.tensor.matmul(gain_ps, lhsT=ident_bf[:], rhs=gain_bf[:], start=True, stop=True)

        state = {}

        def on_pe(k):
            return 0 < k < BLOCKS and k % 8 != 4

        def spread_r2(k):
            ps = bank("r2", 1)
            for q in range(4):
                c = 4 * k + q
                nc.tensor.transpose(ps[:, q * P : (q + 1) * P], r2[:, c : c + 1].to_broadcast([P, P]), ident[:])
            state["r2", k] = ps

        def pre_pe(k, t):
            if not on_pe(k):
                return
            b = k // 8
            ps = bank("pp", 2)
            nc.tensor.matmul(ps[:], lhsT=lhs[b][:, t, :], rhs=select[:, k % 8, :], start=True, stop=True)
            state["pp", k, t] = ps
            if k % 8 == 7 and t == 1 and b < 2:
                load_r2_row(b + 2)

        def pre_v(k):
            b = k // 8
            s = work.tile([P, T4, 512], F32, name="s", tag="s")
            ps = state["r2", k]
            for t in range(2 if on_pe(k) else 0, T4):
                nc.vector.scalar_tensor_tensor(
                    s[:, t, :].rearrange("p (i j) -> p i j", j=NODES),
                    ps[:].rearrange("p (i j) -> p i j", j=NODES),
                    wr_f[:, t : t + 1],
                    uT[:, t, b * NODES : (b + 1) * NODES].unsqueeze(1).to_broadcast([P, 8, NODES]),
                    ALU.mult,
                    ALU.add,
                )
            state["s", k] = s

        def silu1_pe(k, t):
            if on_pe(k):
                nc.scalar.activation(state["s", k][:, t, :], state["pp", k, t][:], ACT.Silu)

        def silu1_v(k):
            s = state["s", k]
            for t in range(2 if on_pe(k) else 0, T4):
                for i in range(8):
                    e = slice(i * NODES, (i + 1) * NODES)
                    node = k * 8 + i
                    nc.scalar.activation(s[:, t, e], s[:, t, e], ACT.Silu, bias=vT[:, t, node : node + 1])

        def gain(k):
            a = work.tile([P, 2048], BF16, name="a", tag="a", align_bytes=64)
            nc.vector.tensor_tensor(
                a[:].rearrange("p (c i t) -> p c t i", i=4, t=T4),
                state["s", k][:].rearrange("p t (c i) -> p c t i", i=4),
                gain_ps.unsqueeze(1).unsqueeze(3).to_broadcast([P, 128, T4, 4]),
                ALU.mult,
            )
            state["a", k] = a

        def quant(k):
            codes = work.tile([P, 512], U32, name="codes", tag="codes", align_bytes=64)
            plane = work.tile([P, 512], U8, name="plane", tag="plane", align_bytes=64)
            nc.vector.quantize_mx(out=codes[:].bitcast(FP8X4), scales=plane[:], in_=state["a", k][:])
            state["q", k] = (codes, plane)

        def product(k, tiles):
            codes, plane = state["q", k]
            for q in tiles:
                ps = bank("mx", 3)
                nc.tensor.matmul_mx(
                    out=ps[:],
                    lhsT=codes[:, q * P : (q + 1) * P].bitcast(FP8X4),
                    lhsT_scale=plane[:, q * P : (q + 1) * P],
                    rhs=w2w[:].bitcast(FP4X4),
                    rhs_scale=w2s[:],
                    start=True,
                    stop=True,
                )
                state["mx", k, q] = ps

        def silu2(k, tiles):
            if 0 in tiles:
                m = work.tile([P, 4, CHAN], F32, name="m", tag="m", bufs=3)
                state["m", k] = m
            m = state["m", k]
            for q in tiles:
                nc.scalar.activation(m[:, q, :], state["mx", k, q][:], ACT.Silu)

        def gate_dot(k, tiles):
            if 0 in tiles:
                dot = work.tile([P, 4], F32, name="dot", tag="dot")
                state["dot", k] = dot
            dot = state["dot", k]
            for q in tiles:
                junk = work.tile([P, CHAN], F32, name="junk", tag="junk")
                nc.vector.scalar_tensor_tensor(
                    junk[:], state["m", k][:, q, :], 1.0, gw_ps, ALU.mult, ALU.mult, accum_out=dot[:, q : q + 1]
                )

        def gp_tiles(k):
            return (3,)

        def gate_dot_g(k, q):
            prod = work.tile([P, CHAN], F32, name="prod", tag="prod", bufs=3)
            nc.gpsimd.tensor_tensor(prod[:], state["m", k][:, q, :], gw[:], ALU.mult)
            state["prod", k, q] = prod

        def gate_dot_s(k, q):
            junk_s = work.tile([P, CHAN], F32, name="junk_s", tag="junk_s", bufs=1)
            nc.scalar.activation(
                junk_s[:], state["prod", k, q][:], ACT.Copy, accum_out=state["dot", k][:, q : q + 1]
            )

        def gate(k):
            th = work.tile([P, 4], F32, name="th", tag="th")
            nc.scalar.activation(th[:], state["dot", k][:], ACT.Tanh, scale=0.5)
            g = work.tile([P, 4], F32, name="g", tag="g")
            nc.gpsimd.tensor_scalar(g[:], th[:], 1.0, 0.0625, ALU.add, ALU.mult)
            state["g", k] = g
            state["gm", k] = big([P, 4, CHAN], F32, "gm")

        def weigh_s(k, tiles):
            for q in tiles:
                nc.scalar.activation(
                    state["gm", k][:, q, :], state["m", k][:, q, :], ACT.Copy, scale=state["g", k][:, q : q + 1]
                )

        def weigh_g(k, tiles):
            for q in tiles:
                nc.gpsimd.tensor_scalar(
                    state["gm", k][:, q, :], state["m", k][:, q, :], state["g", k][:, q : q + 1], 0.0, ALU.mult, ALU.add
                )

        def weigh_v(k, tiles):
            for q in tiles:
                nc.vector.tensor_scalar(
                    state["gm", k][:, q, :], state["m", k][:, q, :], state["g", k][:, q : q + 1], None, ALU.mult
                )

        groups = [(4 * n, 4) for n in range(7)] + [(28, 2), (30, 1), (31, 1)]

        def add_up(n, slices):
            first, count = groups[n]
            if 0 in slices:
                state["acc", n] = bank("acc", 1) if count == 4 else bank("mx", 3)
            acc = state["acc", n]
            for s in slices:
                for x in range(4 * count):
                    nc.tensor.matmul(
                        acc[:, s * P : (s + 1) * P],
                        lhsT=state["gm", first + x // 4][:, x % 4, s * P : (s + 1) * P],
                        rhs=ident[:],
                        is_transpose=True,
                        start=(x == 0),
                        stop=(x == 4 * count - 1),
                    )

        def collect(n):
            first, count = groups[n]
            b = first // 8
            part = work.tile([P, 512], F32, name="part", tag="part")
            if first % 8 == 0:
                nc.vector.tensor_copy(part[:], state["acc", n][:])
            else:
                nc.vector.tensor_tensor(part[:], state["acc", n][:], state["part"][:], ALU.add)
            state["part"] = part
            if (first + count) % 8 != 0:
                return
            halves = part[:].rearrange("p (s h i) -> p s h i", s=4, h=2)
            if b % 2 == 0:
                oT = work.tile([P, 4, 2, NODES], F32, name="oT", tag="oT", bufs=1)
                state["oT"] = oT
            oT = state["oT"]
            nc.vector.tensor_tensor(oT[:, :, b % 2, :], halves[:, :, 0, :], halves[:, :, 1, :], ALU.add)
            if b % 2 == 1:
                ps = bank("r2", 1)
                for s in range(4):
                    nc.tensor.transpose(
                        ps[:, s * P : (s + 1) * P], oT[:, s].rearrange("p b i -> p (b i)"), ident[:]
                    )
                res = work.tile([P, CHAN], F32, name="res", tag="res", bufs=1)
                nc.scalar.copy(res[:], ps[:])
                nc.sync.dma_start(out=out.flatten_outer_dims()[(b // 2) * P : (b // 2 + 1) * P, :], in_=res[:])

        spread_r2(0)
        pre_v(0)
        silu1_v(0)
        spread_r2(1)
        pre_pe(1, 0)
        pre_pe(1, 1)
        for k in range(BLOCKS):
            nxt = k + 1 < BLOCKS
            if nxt:
                pre_v(k + 1)
            if 2 <= k:
                gate(k - 2)
                weigh_g(k - 2, (0, 1, 2))
            if 1 <= k:
                product(k - 1, (0, 1, 2))
            if nxt:
                silu1_pe(k + 1, 0)
                silu1_pe(k + 1, 1)
            pre_pe(k + 2, 0)
            if 1 <= k:
                silu2(k - 1, (0,))
                product(k - 1, (3,))
                silu2(k - 1, (1, 2, 3))
                gate_dot_g(k - 1, 3)
            pre_pe(k + 2, 1)
            if k + 2 < BLOCKS:
                spread_r2(k + 2)
            if nxt:
                silu1_v(k + 1)
            if 2 <= k:
                weigh_s(k - 2, (3,))
            if 1 <= k <= 4:
                lhs_odd(k - 1)
            if k % 4 == 2 and k >= 10:
                collect((k - 10) // 4)
            if 6 <= k < 30:
                add_up((k - 6) // 4, ((k - 6) % 4,))
            elif k >= 30:
                add_up(6, (0, 1) if k == 30 else (2, 3))
            gain(k)
            if 1 <= k:
                gate_dot(k - 1, (0,))
            quant(k)
            if 1 <= k:
                gate_dot(k - 1, (1, 2))
                gate_dot_s(k - 1, 3)
        product(31, (0, 1, 2))
        gate(30)
        silu2(31, (0,))
        product(31, (3,))
        silu2(31, (1, 2, 3))
        weigh_v(30, (0, 1, 2, 3))
        add_up(7, (0, 1, 2, 3))
        collect(6)
        gate_dot(31, (0, 1, 2, 3))
        add_up(8, (0, 1, 2, 3))
        gate(31)
        collect(7)
        weigh_s(31, (0,))
        weigh_v(31, (1, 2, 3))
        collect(8)
        add_up(9, (0, 1, 2, 3))
        collect(9)
